import numpy as np
import ml_dtypes


def mxq(x, axis, fmt="e4m3"):
    dtype, down = {"e4m3": (ml_dtypes.float8_e4m3fn, 7), "e5m2": (ml_dtypes.float8_e5m2, 14)}[fmt]
    v = np.moveaxis(np.asarray(x, np.float32).astype(ml_dtypes.bfloat16).astype(np.float64), axis, -1)
    blocks = v.reshape(v.shape[:-1] + (-1, 32))
    amax = np.abs(blocks).max(-1, keepdims=True)
    byte = np.maximum(np.where(amax > 0, np.frexp(amax)[1] - 1 + 127, 0) - down, 1)
    scale = np.exp2(byte - 127.0)
    codes = (blocks / scale).astype(np.float32).astype(dtype).astype(np.float64)
    return np.moveaxis((codes * scale).reshape(v.shape), -1, axis)


WIDE = False


def mx_kscale(k):
    if not WIDE:
        return np.ones(k)
    levels = np.array([10, -10, 5, -5, 0])
    if k % 512:
        return np.exp2(np.random.permutation(np.resize(levels, k // 32))).repeat(32)
    a = np.empty((k // 512, 16))
    for p in range(k // 512):
        a[p, :8] = np.random.permutation(np.resize(levels, 8))
        for g in range(8):
            far = levels[np.abs(levels - a[p, g]) >= 10]
            a[p, g + 8] = far[np.random.randint(len(far))]
    return np.exp2(a.ravel()).repeat(32)


def f64(x):
    return np.asarray(x).astype(np.float64)


def striped(idx):
    return np.tile(idx.reshape(-1, 16).T, (8, 1)).astype(np.uint16)


def unstriped(offs):
    return offs[:16].T.reshape(-1).astype(np.int64)


def pack_weight(w):
    k, n = w.shape
    w = f64(np.asarray(w, np.float32).astype(ml_dtypes.bfloat16)).reshape(k // 32, 32, n)
    amax = np.abs(w).max(1)
    byte = np.clip(np.where(amax > 0, np.frexp(amax)[1] - 1 + 127 - 7, 1), 1, 254)
    scaled = (w * np.exp2(127.0 - byte)[:, None, :]).reshape(k, n).astype(np.float32)
    words = np.ascontiguousarray(scaled.reshape(k // 512, 128, 4, n).transpose(0, 1, 3, 2)).astype(ml_dtypes.float8_e4m3fn).view(np.uint8)
    return words, np.ascontiguousarray(byte.astype(np.uint8).reshape(k // 512, 16, n))


def unpack_weight(words, scales):
    g, p, n, _ = words.shape
    vals = np.ascontiguousarray(words).view(ml_dtypes.float8_e4m3fn).astype(np.float64) * np.repeat(np.exp2(scales.astype(np.float64) - 127.0), 8, axis=1)[..., None]
    return vals.transpose(0, 1, 3, 2).reshape(g * 512, n)


def planes(y):
    n, m = y.shape
    v = y.astype(np.float32).astype(ml_dtypes.bfloat16).astype(np.float64).reshape(n // 32, 32, m)
    top = np.abs(v).max(1)
    byte = np.clip(np.where(top > 0, np.frexp(top)[1] - 1 + 127 - 7, 1), 1, 254)
    codes = (v * np.exp2(127.0 - byte)[:, None, :]).reshape(n, m).astype(np.float32).astype(ml_dtypes.float8_e4m3fn).view(np.uint8)
    words = codes.reshape(n // 512, 128, 4, m).transpose(0, 1, 3, 2)
    return np.ascontiguousarray(words), np.ascontiguousarray(byte.astype(np.uint8).reshape(n // 512, 16, m))


def sigmoid(v):
    return 1.0 / (1.0 + np.exp(-np.maximum(v, -700.0)))


def gelu(v):
    return 0.5 * v * (1.0 + np.tanh(np.sqrt(2.0 / np.pi) * (v + 0.044715 * v**3)))


K, T, S, W, H = 512, 2048, 512, 1024, 512


def setup_inputs():
    n = np.random.standard_normal
    s = mx_kscale(K)[:, None]
    u = mx_kscale(H)
    packed_xT = pack_weight(n((K, T)) * s)
    packed_eT = pack_weight(n((K, W)) * s)
    packed_w3 = pack_weight(n((H, H)) / np.sqrt(H) / u[:, None])
    return {
        "x_words": packed_xT[0],
        "x_scales": packed_xT[1],
        "e_words": packed_eT[0],
        "e_scales": packed_eT[1],
        "w1": (n((K, H)) / np.sqrt(2 * K) / s * u).astype(np.float32),
        "w2": (n((K, H)) / np.sqrt(2 * K) / s * u).astype(np.float32),
        "w3_words": packed_w3[0],
        "w3_scales": packed_w3[1],
        "skip": (n((H, S)) * u[:, None]).astype(np.float32),
        "offs": striped(np.random.permutation(T)[:S]),
        "tok": striped(np.random.permutation(W)[:S]),
    }


def reference(x_words, x_scales, e_words, e_scales, w1, w2, w3_words, w3_scales, skip, offs, tok):
    xq = unpack_weight(x_words, x_scales)[:, unstriped(offs)]
    e_tok = unpack_weight(e_words, e_scales)[:, unstriped(tok)]
    h = gelu(mxq(f64(w1), 0, "e4m3").T @ xq + mxq(f64(w2), 0, "e4m3").T @ e_tok)
    g = sigmoid(unpack_weight(w3_words, w3_scales).T @ mxq(h, 0, "e4m3"))
    out_0 = f64(skip) + g * (h - f64(skip))
    return (out_0,) + planes(out_0)

@@ -1,0 +1,227 @@
+from contextlib import ExitStack
+
+import concourse.mybir as mybir
+
+F32 = mybir.dt.float32
+BF16 = mybir.dt.bfloat16
+I32 = mybir.dt.int32
+U32 = mybir.dt.uint32
+U16 = mybir.dt.uint16
+U8 = mybir.dt.uint8
+FP8X4 = mybir.dt.float8_e4m3fn_x4
+ACT = mybir.ActivationFunctionType
+ALU = mybir.AluOpType
+
+P = 128
+PACK = 4
+K, T, S, W, H = 512, 2048, 512, 1024, 512
+CH = 128
+NCH = S // CH
+FLOPS = 3 * 2 * 512 * 512 * 512
+H_CAST = "SVSS"
+OUT_CAST = "SSSV"
+ORDER = "mm10 mm11 gb0 gf0 mm12 qh0 gf1 dd0 gf2 gb1 mm13 dd1 gb2 qh1 th0 dd2 gf3 qh2 mm0 gb3 dd3 th1 qh3 oo0 th2 mm1 oc0 mm2 th3 oo1 mm3 oc1 oo2 oo3 oc2 qo0 qo1 oc3 qo2 qo3"
+
+
+def tile_picked_zhwy_gelu_po_kernel(
+    tc, x_words, x_scales, e_words, e_scales, w1, w2, w3_words, w3_scales, skip, offs, tok, out_0, out_1, out_2
+):
+    nc = tc.nc
+    with ExitStack() as ctx:
+        lists = ctx.enter_context(tc.tile_pool(name="lists", bufs=1))
+        keep = ctx.enter_context(tc.tile_pool(name="keep", bufs=1))
+        psum = ctx.enter_context(tc.psum_pool(name="psum", bufs=1))
+
+        def sb(shape, dtype, name, tag=None):
+            return keep.tile(shape, dtype, name=name, tag=tag or name, align_bytes=64)
+
+        def words_view(dram):
+            return dram[0].rearrange("p c r -> p (c r)").bitcast(I32)
+
+        def load_scales(queue, plane, dram):
+            rows = dram[0].rearrange("(q r) c -> r q c", r=4)
+            for r in range(4):
+                queue.dma_start(out=plane[r:P:32, :].bitcast(I32), in_=rows[r].bitcast(I32))
+
+        offs_sb = lists.tile([P, S // 16], U16, name="offs_sb")
+        tok_sb = lists.tile([P, S // 16], U16, name="tok_sb")
+        nc.sync.dma_start(offs_sb[:], offs)
+        nc.sync.dma_start(tok_sb[:], tok)
+
+        xs_tab = sb([P, T], U8, "xs_tab", "slot_c")
+        w3s_raw = sb([P, H], U8, "w3s_raw")
+        w1_raw = sb([P, PACK, H], F32, "w1_raw", "slot_a")
+        nc.sync.dma_start(out=w1_raw[:], in_=w1.rearrange("(p j) c -> p j c", j=PACK))
+        nc.vector.memset(xs_tab[:].bitcast(I32), 0)
+        load_scales(nc.scalar, xs_tab, x_scales)
+        nc.vector.memset(w3s_raw[:].bitcast(I32), 0)
+        load_scales(nc.gpsimd, w3s_raw, w3_scales)
+
+        warm_in = sb([P, 1], F32, "warm_in", "slot_b")
+        warm_out = sb([P, 1], F32, "warm_out", "slot_d")
+        nc.vector.memset(warm_in[:], 0.0)
+        nc.scalar.activation(warm_out[:], warm_in[:], ACT.Gelu_apprx_tanh)
+
+        w2_raw = sb([P, PACK, H], F32, "w2_raw", "slot_b")
+        nc.sync.dma_start(out=w2_raw[:], in_=w2.rearrange("(p j) c -> p j c", j=PACK))
+        es_tab = sb([P, W], U8, "es_tab", "slot_d")
+        nc.vector.memset(es_tab[:].bitcast(I32), 0)
+        load_scales(nc.sync, es_tab, e_scales)
+
+        def deal_and_round(raw, name, split):
+            grouped = sb([P, H * PACK], BF16, name)
+            src = raw[:].rearrange("p j (m t) -> p m t j", t=PACK)
+            dst = grouped[:].rearrange("p (t m j) -> p m t j", t=PACK, j=PACK)
+            nc.vector.tensor_copy(out=dst[:, 0:split], in_=src[:, 0:split])
+            nc.scalar.copy(out=dst[:, split:P], in_=src[:, split:P])
+            return grouped
+
+        w_codes = [sb([P, H], U32, "w1_codes"), sb([P, H], U32, "w2_codes")]
+        w_scales = [sb([P, H], U8, "w1_scales"), sb([P, H], U8, "w2_scales")]
+
+        xs = sb([P, S], U8, "xs")
+        nc.vector.tensor_copy(xs[:], xs_tab[:].indirect(offs_sb[:]))
+        xw_tab = sb([P, T], U32, "xw_tab", "slot_c")
+        nc.sync.dma_start(out=xw_tab[:].bitcast(I32), in_=words_view(x_words))
+
+        w1_bf = deal_and_round(w1_raw, "w1_bf", 64)
+        ew_tab = sb([P, W], U32, "ew_tab", "slot_a")
+        nc.sync.dma_start(out=ew_tab[:].bitcast(I32), in_=words_view(e_words))
+        nc.vector.quantize_mx(out=w_codes[0][:].bitcast(FP8X4), scales=w_scales[0][:], in_=w1_bf[:])
+
+        w2_bf = deal_and_round(w2_raw, "w2_bf", 48)
+        es = sb([P, S], U8, "es")
+        nc.vector.tensor_copy(es[:], es_tab[:].indirect(tok_sb[:]))
+        nc.vector.quantize_mx(out=w_codes[1][:].bitcast(FP8X4), scales=w_scales[1][:], in_=w2_bf[:])
+
+        w3w_raw = sb([P, H], I32, "w3w_raw", "slot_d")
+        nc.sync.dma_start(out=w3w_raw[:], in_=words_view(w3_words))
+        skip_rows = skip.rearrange("(p t) c -> p t c", t=PACK)
+        skip_a = sb([P, PACK, 2 * CH], F32, "skip_a", "slot_b")
+        nc.sync.dma_start(out=skip_a[:], in_=skip_rows[:, :, 0 : 2 * CH])
+
+        def gather_words(table, offsets, first, n, name):
+            piece = sb([P, n], U32, name)
+            nc.vector.tensor_copy(piece[:], table[:].indirect(offsets[:, first // 16 : (first + n) // 16]))
+            return [piece[:, c * CH : (c + 1) * CH] for c in range(n // CH)]
+
+        xw = gather_words(xw_tab, offs_sb, 0, 2 * CH, "xw_a")
+        ew = gather_words(ew_tab, tok_sb, 0, CH, "ew_a")
+        ew = ew + gather_words(ew_tab, tok_sb, CH, CH, "ew_b")
+        xw = xw + gather_words(xw_tab, offs_sb, 2 * CH, 2 * CH, "xw_b")
+        skip_b = sb([P, PACK, 2 * CH], F32, "skip_b", "slot_c")
+        nc.sync.dma_start(out=skip_b[:], in_=skip_rows[:, :, 2 * CH : 4 * CH])
+        skip_sb = [t[:, :, c * CH : (c + 1) * CH] for t in (skip_a, skip_b) for c in range(2)]
+
+        ew = ew + gather_words(ew_tab, tok_sb, 2 * CH, 2 * CH, "ew_c")
+        w3w = sb([P, H], I32, "w3w")
+        nc.vector.tensor_copy(
+            out=w3w[:].rearrange("p (t m) -> p m t", t=PACK), in_=w3w_raw[:].rearrange("p (m t) -> p m t", t=PACK)
+        )
+
+        w3s = sb([P, H], U8, "w3s", "w2_bf")
+        nc.vector.tensor_copy(
+            out=w3s[:].rearrange("p (t m) -> p m t", t=PACK), in_=w3s_raw[:].rearrange("p (m t) -> p m t", t=PACK)
+        )
+
+        out_rows = out_0.rearrange("(p t) c -> p t c", t=PACK)
+        out_codes = sb([P, S], U32, "out_codes")
+        out_scales = sb([P, S], U8, "out_scales")
+        st = [dict() for c in range(NCH)]
+
+        def cols(c):
+            return slice(c * CH, (c + 1) * CH)
+
+        def interleave(engine, dst, src):
+            d = dst[:].rearrange("p (c i t) -> p c t i", i=4, t=PACK)
+            s = src[:].rearrange("p t (c i) -> p c t i", i=4)
+            if engine == "V":
+                nc.vector.tensor_copy(out=d, in_=s)
+            else:
+                nc.scalar.copy(out=d, in_=s)
+
+        def mm1(c):
+            pre = psum.tile([P, PACK, CH], F32, name="pre%d" % c)
+            for t in range(PACK):
+                for i, (mw, ms) in enumerate(((xw[c], xs), (ew[c], es))):
+                    nc.tensor.matmul_mx(
+                        out=pre[:, t, :],
+                        lhsT=w_codes[i][:, cols(t)].bitcast(FP8X4),
+                        lhsT_scale=w_scales[i][:, cols(t)],
+                        rhs=mw.bitcast(FP8X4),
+                        rhs_scale=ms[:, cols(c)],
+                        start=(i == 0),
+                        stop=(i == 1),
+                    )
+            st[c]["pre"] = pre
+
+        def gb(c):
+            if H_CAST[c] == "S":
+                st[c]["h_bf"] = sb([P, CH * PACK], BF16, "h_bf%d" % c)
+                nc.scalar.activation(
+                    st[c]["h_bf"][:].rearrange("p (n t) -> p n t", t=PACK),
+                    st[c]["pre"][:].rearrange("p t n -> p n t"),
+                    ACT.Gelu_apprx_tanh,
+                )
+            else:
+                st[c]["h_bf"] = sb([P, CH * PACK], BF16, "h_bf%d" % c)
+                interleave("V", st[c]["h_bf"], st[c]["h"])
+
+        def gf(c):
+            st[c]["h"] = sb([P, PACK, CH], F32, "h%d" % c)
+            nc.scalar.activation(st[c]["h"][:], st[c]["pre"][:], ACT.Gelu_apprx_tanh)
+
+        def qh(c):
+            hc = sb([P, CH], U32, "h_codes%d" % c)
+            hs = sb([P, CH], U8, "h_scales%d" % c)
+            nc.vector.quantize_mx(out=hc[:].bitcast(FP8X4), scales=hs[:], in_=st[c]["h_bf"][:])
+            z = psum.tile([P, PACK, CH], F32, name="z%d" % c)
+            for t in range(PACK):
+                nc.tensor.matmul_mx(
+                    out=z[:, t, :],
+                    lhsT=w3w[:, cols(t)].bitcast(FP8X4),
+                    lhsT_scale=w3s[:, cols(t)],
+                    rhs=hc[:].bitcast(FP8X4),
+                    rhs_scale=hs[:],
+                    start=True,
+                    stop=True,
+                )
+            st[c]["z"] = z
+
+        def th(c):
+            st[c]["th"] = sb([P, PACK, CH], F32, "th%d" % c)
+            nc.scalar.activation(st[c]["th"][:], st[c]["z"][:], ACT.Tanh, scale=0.5)
+
+        def dd(c):
+            st[c]["d"] = sb([P, PACK, CH], F32, "d%d" % c)
+            nc.vector.tensor_tensor(st[c]["d"][:], st[c]["h"][:], skip_sb[c], ALU.subtract)
+
+        def mm(c):
+            st[c]["m"] = sb([P, PACK, CH], F32, "m%d" % c)
+            nc.vector.scalar_tensor_tensor(st[c]["m"][:], st[c]["th"][:], 1.0, st[c]["d"][:], ALU.add, ALU.mult)
+
+        def oo(c):
+            st[c]["o"] = sb([P, PACK, CH], F32, "o%d" % c)
+            nc.vector.scalar_tensor_tensor(st[c]["o"][:], st[c]["m"][:], 0.5, skip_sb[c], ALU.mult, ALU.add)
+            nc.sync.dma_start(out=out_rows[:, :, cols(c)], in_=st[c]["o"][:])
+
+        def oc(c):
+            st[c]["o_bf"] = sb([P, CH * PACK], BF16, "o_bf%d" % c)
+            interleave(OUT_CAST[c], st[c]["o_bf"], st[c]["o"])
+
+        def qo(c):
+            nc.vector.quantize_mx(
+                out=out_codes[:, cols(c)].bitcast(FP8X4), scales=out_scales[:, cols(c)], in_=st[c]["o_bf"][:]
+            )
+
+        steps = dict(mm1=mm1, gb=gb, gf=gf, qh=qh, th=th, dd=dd, mm=mm, oo=oo, oc=oc, qo=qo)
+        for item in ORDER.split():
+            steps[item[:-1]](int(item[-1]))
+            if item == "qo2":
+                nc.sync.dma_start(out=words_view(out_1)[:, 0 : 3 * CH], in_=out_codes[:, 0 : 3 * CH].bitcast(I32))
+        nc.sync.dma_start(out=words_view(out_1)[:, 3 * CH : S], in_=out_codes[:, 3 * CH : S].bitcast(I32))
+        for q in range(4):
+            queue = nc.scalar if q < 2 else nc.sync
+            queue.dma_start(
+                out=out_2[0, 4 * q : 4 * q + 4, :].bitcast(I32), in_=out_scales[32 * q : 32 * q + 4, :].bitcast(I32)
+            )

@@ -18,6 +18,7 @@ K, T, S, W, H = 512, 2048, 512, 1024, 512
 CH = 128
 NCH = S // CH
 FLOPS = 3 * 2 * 512 * 512 * 512
+X_ROW, E_ROW, W3_ROW = 0, 4, 8
 H_CAST = "SVSS"
 OUT_CAST = "SSSV"
 ORDER = "mm10 mm11 gb0 gf0 mm12 qh0 gf1 dd0 gf2 gb1 mm13 dd1 gb2 qh1 th0 dd2 gf3 qh2 mm0 gb3 dd3 th1 qh3 oo0 th2 mm1 oc0 mm2 th3 oo1 mm3 oc1 oo2 oo3 oc2 qo0 qo1 oc3 qo2 qo3"
@@ -38,35 +39,44 @@ def tile_picked_zhwy_gelu_po_kernel(
         def words_view(dram):
             return dram[0].rearrange("p c r -> p (c r)").bitcast(I32)
 
-        def load_scales(queue, plane, dram):
+        def load_scales(plane, dram, row):
             rows = dram[0].rearrange("(q r) c -> r q c", r=4)
             for r in range(4):
-                queue.dma_start(out=plane[r:P:32, :].bitcast(I32), in_=rows[r].bitcast(I32))
+                nc.sync.dma_start(out=plane[row + r : P : 32, :].bitcast(I32), in_=rows[r].bitcast(I32))
 
         offs_sb = lists.tile([P, S // 16], U16, name="offs_sb")
         tok_sb = lists.tile([P, S // 16], U16, name="tok_sb")
+
+        xs_tab = sb([P, T], U8, "xs_tab")
+        es_tab = sb([P, W], U8, "es_tab")
+        w3s_raw = sb([P, H], U8, "w3s_raw")
+        for plane in (xs_tab, es_tab, w3s_raw):
+            nc.gpsimd.memset(plane[:].bitcast(I32), 0)
+        w1_raw = sb([P, PACK, H], F32, "w1_raw")
+        w2_raw = sb([P, PACK, H], F32, "w2_raw")
+        xw_tab = sb([P, T], U32, "xw_tab")
+        ew_tab = sb([P, W], U32, "ew_tab")
+        w3w_raw = sb([P, H], I32, "w3w_raw")
+        skip_a = sb([P, PACK, 2 * CH], F32, "skip_a")
+        skip_b = sb([P, PACK, 2 * CH], F32, "skip_b")
+        skip_rows = skip.rearrange("(p t) c -> p t c", t=PACK)
+        nc.sync.dma_start(out=w1_raw[:], in_=w1.rearrange("(p j) c -> p j c", j=PACK))
         nc.sync.dma_start(offs_sb[:], offs)
         nc.sync.dma_start(tok_sb[:], tok)
+        load_scales(xs_tab, x_scales, X_ROW)
+        nc.sync.dma_start(out=w2_raw[:], in_=w2.rearrange("(p j) c -> p j c", j=PACK))
+        load_scales(es_tab, e_scales, E_ROW)
+        nc.sync.dma_start(out=xw_tab[:].bitcast(I32), in_=words_view(x_words))
+        load_scales(w3s_raw, w3_scales, W3_ROW)
+        nc.sync.dma_start(out=ew_tab[:].bitcast(I32), in_=words_view(e_words))
+        nc.sync.dma_start(out=w3w_raw[:], in_=words_view(w3_words))
+        nc.sync.dma_start(out=skip_a[:], in_=skip_rows[:, :, 0 : 2 * CH])
+        nc.sync.dma_start(out=skip_b[:], in_=skip_rows[:, :, 2 * CH : 4 * CH])
 
-        xs_tab = sb([P, T], U8, "xs_tab", "slot_c")
-        w3s_raw = sb([P, H], U8, "w3s_raw")
-        w1_raw = sb([P, PACK, H], F32, "w1_raw", "slot_a")
-        nc.sync.dma_start(out=w1_raw[:], in_=w1.rearrange("(p j) c -> p j c", j=PACK))
-        nc.vector.memset(xs_tab[:].bitcast(I32), 0)
-        load_scales(nc.scalar, xs_tab, x_scales)
-        nc.vector.memset(w3s_raw[:].bitcast(I32), 0)
-        load_scales(nc.gpsimd, w3s_raw, w3_scales)
-
-        warm_in = sb([P, 1], F32, "warm_in", "slot_b")
-        warm_out = sb([P, 1], F32, "warm_out", "slot_d")
+        warm_in = sb([P, 1], F32, "warm_in")
+        warm_out = sb([P, 1], F32, "warm_out")
         nc.vector.memset(warm_in[:], 0.0)
         nc.scalar.activation(warm_out[:], warm_in[:], ACT.Gelu_apprx_tanh)
-
-        w2_raw = sb([P, PACK, H], F32, "w2_raw", "slot_b")
-        nc.sync.dma_start(out=w2_raw[:], in_=w2.rearrange("(p j) c -> p j c", j=PACK))
-        es_tab = sb([P, W], U8, "es_tab", "slot_d")
-        nc.vector.memset(es_tab[:].bitcast(I32), 0)
-        load_scales(nc.sync, es_tab, e_scales)
 
         def deal_and_round(raw, name, split):
             grouped = sb([P, H * PACK], BF16, name)
@@ -81,24 +91,26 @@ def tile_picked_zhwy_gelu_po_kernel(
 
         xs = sb([P, S], U8, "xs")
         nc.vector.tensor_copy(xs[:], xs_tab[:].indirect(offs_sb[:]))
-        xw_tab = sb([P, T], U32, "xw_tab", "slot_c")
-        nc.sync.dma_start(out=xw_tab[:].bitcast(I32), in_=words_view(x_words))
 
         w1_bf = deal_and_round(w1_raw, "w1_bf", 64)
-        ew_tab = sb([P, W], U32, "ew_tab", "slot_a")
-        nc.sync.dma_start(out=ew_tab[:].bitcast(I32), in_=words_view(e_words))
         nc.vector.quantize_mx(out=w_codes[0][:].bitcast(FP8X4), scales=w_scales[0][:], in_=w1_bf[:])
 
         w2_bf = deal_and_round(w2_raw, "w2_bf", 48)
         es = sb([P, S], U8, "es")
         nc.vector.tensor_copy(es[:], es_tab[:].indirect(tok_sb[:]))
         nc.vector.quantize_mx(out=w_codes[1][:].bitcast(FP8X4), scales=w_scales[1][:], in_=w2_bf[:])
+        pe_warm = psum.tile([P, H], F32, name="pe_warm", tag="z3")
+        for i in range(3):
+            nc.tensor.matmul_mx(
+                out=pe_warm[:],
+                lhsT=w_codes[0][:, 0:P].bitcast(FP8X4),
+                lhsT_scale=w_scales[0][:, 0:P],
+                rhs=w_codes[1][:].bitcast(FP8X4),
+                rhs_scale=w_scales[1][:],
+                start=True,
+                stop=True,
+            )
 
-        w3w_raw = sb([P, H], I32, "w3w_raw", "slot_d")
-        nc.sync.dma_start(out=w3w_raw[:], in_=words_view(w3_words))
-        skip_rows = skip.rearrange("(p t) c -> p t c", t=PACK)
-        skip_a = sb([P, PACK, 2 * CH], F32, "skip_a", "slot_b")
-        nc.sync.dma_start(out=skip_a[:], in_=skip_rows[:, :, 0 : 2 * CH])
 
         def gather_words(table, offsets, first, n, name):
             piece = sb([P, n], U32, name)
@@ -109,8 +121,6 @@ def tile_picked_zhwy_gelu_po_kernel(
         ew = gather_words(ew_tab, tok_sb, 0, CH, "ew_a")
         ew = ew + gather_words(ew_tab, tok_sb, CH, CH, "ew_b")
         xw = xw + gather_words(xw_tab, offs_sb, 2 * CH, 2 * CH, "xw_b")
-        skip_b = sb([P, PACK, 2 * CH], F32, "skip_b", "slot_c")
-        nc.sync.dma_start(out=skip_b[:], in_=skip_rows[:, :, 2 * CH : 4 * CH])
         skip_sb = [t[:, :, c * CH : (c + 1) * CH] for t in (skip_a, skip_b) for c in range(2)]
 
         ew = ew + gather_words(ew_tab, tok_sb, 2 * CH, 2 * CH, "ew_c")
@@ -119,7 +129,7 @@ def tile_picked_zhwy_gelu_po_kernel(
             out=w3w[:].rearrange("p (t m) -> p m t", t=PACK), in_=w3w_raw[:].rearrange("p (m t) -> p m t", t=PACK)
         )
 
-        w3s = sb([P, H], U8, "w3s", "w2_bf")
+        w3s = sb([P, H], U8, "w3s")
         nc.vector.tensor_copy(
             out=w3s[:].rearrange("p (t m) -> p m t", t=PACK), in_=w3s_raw[:].rearrange("p (m t) -> p m t", t=PACK)
         )
@@ -143,13 +153,13 @@ def tile_picked_zhwy_gelu_po_kernel(
         def mm1(c):
             pre = psum.tile([P, PACK, CH], F32, name="pre%d" % c)
             for t in range(PACK):
-                for i, (mw, ms) in enumerate(((xw[c], xs), (ew[c], es))):
+                for i, (mw, ms) in enumerate(((xw[c], xs[X_ROW:P, cols(c)]), (ew[c], es[E_ROW:P, cols(c)]))):
                     nc.tensor.matmul_mx(
                         out=pre[:, t, :],
                         lhsT=w_codes[i][:, cols(t)].bitcast(FP8X4),
                         lhsT_scale=w_scales[i][:, cols(t)],
                         rhs=mw.bitcast(FP8X4),
-                        rhs_scale=ms[:, cols(c)],
+                        rhs_scale=ms,
                         start=(i == 0),
                         stop=(i == 1),
                     )
@@ -175,12 +185,12 @@ def tile_picked_zhwy_gelu_po_kernel(
             hc = sb([P, CH], U32, "h_codes%d" % c)
             hs = sb([P, CH], U8, "h_scales%d" % c)
             nc.vector.quantize_mx(out=hc[:].bitcast(FP8X4), scales=hs[:], in_=st[c]["h_bf"][:])
-            z = psum.tile([P, PACK, CH], F32, name="z%d" % c)
+            z = psum.tile([P, PACK, CH], F32, name="z%d" % c, tag="z%d" % c)
             for t in range(PACK):
                 nc.tensor.matmul_mx(
                     out=z[:, t, :],
                     lhsT=w3w[:, cols(t)].bitcast(FP8X4),
-                    lhsT_scale=w3s[:, cols(t)],
+                    lhsT_scale=w3s[W3_ROW:P, cols(t)],
                     rhs=hc[:].bitcast(FP8X4),
                     rhs_scale=hs[:],
                     start=True,

@@ -14,14 +14,22 @@ ALU = mybir.AluOpType
 
 P = 128
 PACK = 4
-K, T, S, W, H = 512, 2048, 512, 1024, 512
-CH = 128
-NCH = S // CH
-FLOPS = 3 * 2 * 512 * 512 * 512
+STATES, VOCAB, POSITIONS, HIDDEN = 2048, 1024, 512, 512
+CHUNK = 128
+CHUNKS = POSITIONS // CHUNK
+FLOPS = 3 * 2 * 512 * HIDDEN * POSITIONS
+
 X_ROW, E_ROW, W3_ROW = 0, 4, 8
-H_CAST = "SVSS"
-OUT_CAST = "SSSV"
-ORDER = "mm10 mm11 gb0 gf0 mm12 qh0 gf1 dd0 gf2 gb1 mm13 dd1 gb2 qh1 th0 dd2 gf3 qh2 mm0 gb3 dd3 th1 qh3 oo0 th2 mm1 oc0 mm2 th3 oo1 mm3 oc1 oo2 oo3 oc2 qo0 qo1 oc3 qo2 qo3"
+W1_ON_VECTOR, W2_ON_VECTOR = 64, 48
+H_ROUNDED_ON_VECTOR, OUT_ROUNDED_ON_VECTOR = (1,), (3,)
+WARM_UP_PASSES = 2
+STEPS = (
+    "layer1:0 gather_x_rest:2 layer1:1 round_h:0 gelu:0 layer1:2 gate:0 gelu:1 layer1:3 diff:0 gelu:2 round_h:1 "
+    "round_h:2 diff:1 "
+    "tanh:0 gate:1 diff:2 gelu:3 gate:2 scale:0 round_h:3 diff:3 tanh:1 gate:3 tanh:2 result:0 scale:1 round_out:0 "
+    "scale:2 tanh:3 result:1 scale:3 round_out:1 result:2 result:3 round_out:2 quantise_out:0 quantise_out:1 "
+    "round_out:3 quantise_out:2 quantise_out:3"
+)
 
 
 def tile_picked_zhwy_gelu_po_kernel(
@@ -33,203 +41,220 @@ def tile_picked_zhwy_gelu_po_kernel(
         keep = ctx.enter_context(tc.tile_pool(name="keep", bufs=1))
         psum = ctx.enter_context(tc.psum_pool(name="psum", bufs=1))
 
-        def sb(shape, dtype, name, tag=None):
-            return keep.tile(shape, dtype, name=name, tag=tag or name, align_bytes=64)
+        def sbuf(shape, dtype, name, after=None):
+            return keep.tile(shape, dtype, name=name, tag=after or name, align_bytes=64)
+
+        def span(i, width=CHUNK):
+            return slice(i * width, (i + 1) * width)
 
         def words_view(dram):
             return dram[0].rearrange("p c r -> p (c r)").bitcast(I32)
 
-        def load_scales(plane, dram, row):
+        def load_scales(clear_on, tile, dram, row):
+            clear_on.memset(tile[:].bitcast(I32), 0)
             rows = dram[0].rearrange("(q r) c -> r q c", r=4)
             for r in range(4):
-                nc.sync.dma_start(out=plane[row + r : P : 32, :].bitcast(I32), in_=rows[r].bitcast(I32))
+                nc.sync.dma_start(out=tile[row + r : P : 32, :].bitcast(I32), in_=rows[r].bitcast(I32))
 
-        offs_sb = lists.tile([P, S // 16], U16, name="offs_sb")
-        tok_sb = lists.tile([P, S // 16], U16, name="tok_sb")
+        def load_weight(tile, w):
+            nc.sync.dma_start(out=tile[:], in_=w.rearrange("(p j) c -> p j c", j=PACK))
 
-        xs_tab = sb([P, T], U8, "xs_tab")
-        es_tab = sb([P, W], U8, "es_tab")
-        w3s_raw = sb([P, H], U8, "w3s_raw")
-        for plane in (xs_tab, es_tab, w3s_raw):
-            nc.gpsimd.memset(plane[:].bitcast(I32), 0)
-        w1_raw = sb([P, PACK, H], F32, "w1_raw")
-        w2_raw = sb([P, PACK, H], F32, "w2_raw")
-        xw_tab = sb([P, T], U32, "xw_tab")
-        ew_tab = sb([P, W], U32, "ew_tab")
-        w3w_raw = sb([P, H], I32, "w3w_raw")
-        skip_a = sb([P, PACK, 2 * CH], F32, "skip_a")
-        skip_b = sb([P, PACK, 2 * CH], F32, "skip_b")
-        skip_rows = skip.rearrange("(p t) c -> p t c", t=PACK)
-        nc.sync.dma_start(out=w1_raw[:], in_=w1.rearrange("(p j) c -> p j c", j=PACK))
+        def round_and_deal_weight(raw, name, on_vector):
+            rounded = sbuf([P, HIDDEN * PACK], BF16, name)
+            src = raw[:].rearrange("p j (m t) -> p m t j", t=PACK)
+            dst = rounded[:].rearrange("p (t m j) -> p m t j", t=PACK, j=PACK)
+            nc.vector.tensor_copy(out=dst[:, 0:on_vector], in_=src[:, 0:on_vector])
+            nc.scalar.copy(out=dst[:, on_vector:P], in_=src[:, on_vector:P])
+            return rounded
+
+        def deal_columns(dealt, raw):
+            nc.vector.tensor_copy(
+                out=dealt[:].rearrange("p (t m) -> p m t", t=PACK), in_=raw[:].rearrange("p (m t) -> p m t", t=PACK)
+            )
+
+        def gather_words(table, offsets, first_chunk, chunks, name, after=None):
+            picked = sbuf([P, chunks * CHUNK], U32, name, after)
+            columns = slice(first_chunk * CHUNK // 16, (first_chunk + chunks) * CHUNK // 16)
+            nc.vector.tensor_copy(picked[:], table[:].indirect(offsets[:, columns]))
+            return [picked[:, span(c)] for c in range(chunks)]
+
+        def round_and_interleave(on_vector, dst, src):
+            dst_view = dst[:].rearrange("p (c i t) -> p c t i", i=4, t=PACK)
+            src_view = src[:].rearrange("p t (c i) -> p c t i", i=4)
+            if on_vector:
+                nc.vector.tensor_copy(out=dst_view, in_=src_view)
+            else:
+                nc.scalar.copy(out=dst_view, in_=src_view)
+
+        w1_raw = sbuf([P, PACK, HIDDEN], F32, "w1_raw")
+        load_weight(w1_raw, w1)
+        offs_sb = lists.tile([P, POSITIONS // 16], U16, name="offs_sb")
+        tok_sb = lists.tile([P, POSITIONS // 16], U16, name="tok_sb")
         nc.sync.dma_start(offs_sb[:], offs)
         nc.sync.dma_start(tok_sb[:], tok)
-        load_scales(xs_tab, x_scales, X_ROW)
-        nc.sync.dma_start(out=w2_raw[:], in_=w2.rearrange("(p j) c -> p j c", j=PACK))
-        load_scales(es_tab, e_scales, E_ROW)
-        nc.sync.dma_start(out=xw_tab[:].bitcast(I32), in_=words_view(x_words))
-        load_scales(w3s_raw, w3_scales, W3_ROW)
-        nc.sync.dma_start(out=ew_tab[:].bitcast(I32), in_=words_view(e_words))
-        nc.sync.dma_start(out=w3w_raw[:], in_=words_view(w3_words))
-        nc.sync.dma_start(out=skip_a[:], in_=skip_rows[:, :, 0 : 2 * CH])
-        nc.sync.dma_start(out=skip_b[:], in_=skip_rows[:, :, 2 * CH : 4 * CH])
+        e_scale_table = sbuf([P, VOCAB], U8, "e_scale_table")
+        load_scales(nc.gpsimd, e_scale_table, e_scales, E_ROW)
+        w2_raw = sbuf([P, PACK, HIDDEN], F32, "w2_raw")
+        load_weight(w2_raw, w2)
+        x_scale_table = sbuf([P, STATES], U8, "x_scale_table")
+        load_scales(nc.vector, x_scale_table, x_scales, X_ROW)
+        x_word_table = sbuf([P, STATES], U32, "x_word_table")
+        nc.sync.dma_start(out=x_word_table[:].bitcast(I32), in_=words_view(x_words))
+        w3_scales_raw = sbuf([P, HIDDEN], U8, "w3_scales_raw")
+        load_scales(nc.gpsimd, w3_scales_raw, w3_scales, W3_ROW)
+        e_word_table = sbuf([P, VOCAB], U32, "e_word_table")
+        nc.sync.dma_start(out=e_word_table[:].bitcast(I32), in_=words_view(e_words))
+        w3_words_raw = sbuf([P, HIDDEN], I32, "w3_words_raw")
+        nc.sync.dma_start(out=w3_words_raw[:], in_=words_view(w3_words))
+        skip_rows = skip.rearrange("(p t) c -> p t c", t=PACK)
+        skip_sb = []
+        for half in range(2):
+            skip_half = sbuf([P, PACK, 2 * CHUNK], F32, "skip_half%d" % half)
+            nc.sync.dma_start(out=skip_half[:], in_=skip_rows[:, :, span(half, 2 * CHUNK)])
+            skip_sb.extend(skip_half[:, :, span(c)] for c in range(2))
 
-        warm_in = sb([P, 1], F32, "warm_in")
-        warm_out = sb([P, 1], F32, "warm_out")
-        nc.vector.memset(warm_in[:], 0.0)
-        nc.scalar.activation(warm_out[:], warm_in[:], ACT.Gelu_apprx_tanh)
+        w1_rounded = round_and_deal_weight(w1_raw, "w1_rounded", W1_ON_VECTOR)
+        e_picked_scales = sbuf([P, POSITIONS], U8, "e_picked_scales")
+        nc.vector.tensor_copy(e_picked_scales[:], e_scale_table[:].indirect(tok_sb[:]))
+        w1_codes = sbuf([P, HIDDEN], U32, "w1_codes")
+        w1_scales = sbuf([P, HIDDEN], U8, "w1_scales", after="e_scale_table")
+        nc.vector.quantize_mx(out=w1_codes[:].bitcast(FP8X4), scales=w1_scales[:], in_=w1_rounded[:])
 
-        def deal_and_round(raw, name, split):
-            grouped = sb([P, H * PACK], BF16, name)
-            src = raw[:].rearrange("p j (m t) -> p m t j", t=PACK)
-            dst = grouped[:].rearrange("p (t m j) -> p m t j", t=PACK, j=PACK)
-            nc.vector.tensor_copy(out=dst[:, 0:split], in_=src[:, 0:split])
-            nc.scalar.copy(out=dst[:, split:P], in_=src[:, split:P])
-            return grouped
+        w2_rounded = round_and_deal_weight(w2_raw, "w2_rounded", W2_ON_VECTOR)
+        x_picked_scales = sbuf([P, POSITIONS], U8, "x_picked_scales")
+        nc.vector.tensor_copy(x_picked_scales[:], x_scale_table[:].indirect(offs_sb[:]))
+        w2_codes = sbuf([P, HIDDEN], U32, "w2_codes")
+        w2_scales = sbuf([P, HIDDEN], U8, "w2_scales", after="x_scale_table")
+        nc.vector.quantize_mx(out=w2_codes[:].bitcast(FP8X4), scales=w2_scales[:], in_=w2_rounded[:])
 
-        w_codes = [sb([P, H], U32, "w1_codes"), sb([P, H], U32, "w2_codes")]
-        w_scales = [sb([P, H], U8, "w1_scales"), sb([P, H], U8, "w2_scales")]
-
-        xs = sb([P, S], U8, "xs")
-        nc.vector.tensor_copy(xs[:], xs_tab[:].indirect(offs_sb[:]))
-
-        w1_bf = deal_and_round(w1_raw, "w1_bf", 64)
-        nc.vector.quantize_mx(out=w_codes[0][:].bitcast(FP8X4), scales=w_scales[0][:], in_=w1_bf[:])
-
-        w2_bf = deal_and_round(w2_raw, "w2_bf", 48)
-        es = sb([P, S], U8, "es")
-        nc.vector.tensor_copy(es[:], es_tab[:].indirect(tok_sb[:]))
-        nc.vector.quantize_mx(out=w_codes[1][:].bitcast(FP8X4), scales=w_scales[1][:], in_=w2_bf[:])
-        pe_warm = psum.tile([P, H], F32, name="pe_warm", tag="z3")
-        for i in range(3):
+        warm_bank = psum.tile([P, HIDDEN], F32, name="warm_bank", tag="z%d" % (CHUNKS - 1))
+        for i in range(WARM_UP_PASSES):
             nc.tensor.matmul_mx(
-                out=pe_warm[:],
-                lhsT=w_codes[0][:, 0:P].bitcast(FP8X4),
-                lhsT_scale=w_scales[0][:, 0:P],
-                rhs=w_codes[1][:].bitcast(FP8X4),
-                rhs_scale=w_scales[1][:],
+                out=warm_bank[:],
+                lhsT=w1_codes[:, 0:P].bitcast(FP8X4),
+                lhsT_scale=w1_scales[:, 0:P],
+                rhs=w2_codes[:].bitcast(FP8X4),
+                rhs_scale=w2_scales[:],
                 start=True,
                 stop=True,
             )
 
-
-        def gather_words(table, offsets, first, n, name):
-            piece = sb([P, n], U32, name)
-            nc.vector.tensor_copy(piece[:], table[:].indirect(offsets[:, first // 16 : (first + n) // 16]))
-            return [piece[:, c * CH : (c + 1) * CH] for c in range(n // CH)]
-
-        xw = gather_words(xw_tab, offs_sb, 0, 2 * CH, "xw_a")
-        ew = gather_words(ew_tab, tok_sb, 0, CH, "ew_a")
-        ew = ew + gather_words(ew_tab, tok_sb, CH, CH, "ew_b")
-        xw = xw + gather_words(xw_tab, offs_sb, 2 * CH, 2 * CH, "xw_b")
-        skip_sb = [t[:, :, c * CH : (c + 1) * CH] for t in (skip_a, skip_b) for c in range(2)]
-
-        ew = ew + gather_words(ew_tab, tok_sb, 2 * CH, 2 * CH, "ew_c")
-        w3w = sb([P, H], I32, "w3w")
-        nc.vector.tensor_copy(
-            out=w3w[:].rearrange("p (t m) -> p m t", t=PACK), in_=w3w_raw[:].rearrange("p (m t) -> p m t", t=PACK)
-        )
-
-        w3s = sb([P, H], U8, "w3s")
-        nc.vector.tensor_copy(
-            out=w3s[:].rearrange("p (t m) -> p m t", t=PACK), in_=w3s_raw[:].rearrange("p (m t) -> p m t", t=PACK)
-        )
+        x_picked = gather_words(x_word_table, offs_sb, 0, 2, "x_picked0")
+        w3_dealt_scales = sbuf([P, HIDDEN], U8, "w3_dealt_scales")
+        deal_columns(w3_dealt_scales, w3_scales_raw)
+        e_picked = gather_words(e_word_table, tok_sb, 0, 1, "e_picked0")
+        e_picked.extend(gather_words(e_word_table, tok_sb, 1, 1, "e_picked1"))
+        e_picked.extend(gather_words(e_word_table, tok_sb, 2, 2, "e_picked2"))
+        w3_codes = sbuf([P, HIDDEN], I32, "w3_codes", after="e_word_table")
+        deal_columns(w3_codes, w3_words_raw)
 
         out_rows = out_0.rearrange("(p t) c -> p t c", t=PACK)
-        out_codes = sb([P, S], U32, "out_codes")
-        out_scales = sb([P, S], U8, "out_scales")
-        st = [dict() for c in range(NCH)]
+        out_codes = sbuf([P, POSITIONS], U32, "out_codes")
+        out_scales = sbuf([P, POSITIONS], U8, "out_scales")
+        made = {}
 
-        def cols(c):
-            return slice(c * CH, (c + 1) * CH)
+        def chunk_tile(what, c, dtype):
+            shape = [P, PACK, CHUNK] if dtype == F32 else [P, CHUNK * PACK]
+            made[what, c] = sbuf(shape, dtype, "%s%d" % (what, c))
+            return made[what, c]
 
-        def interleave(engine, dst, src):
-            d = dst[:].rearrange("p (c i t) -> p c t i", i=4, t=PACK)
-            s = src[:].rearrange("p t (c i) -> p c t i", i=4)
-            if engine == "V":
-                nc.vector.tensor_copy(out=d, in_=s)
-            else:
-                nc.scalar.copy(out=d, in_=s)
-
-        def mm1(c):
-            pre = psum.tile([P, PACK, CH], F32, name="pre%d" % c)
+        def layer1(c):
+            pre = psum.tile([P, PACK, CHUNK], F32, name="pre%d" % c)
+            products = (
+                (w1_codes, w1_scales, x_picked[c], x_picked_scales[X_ROW:P, span(c)]),
+                (w2_codes, w2_scales, e_picked[c], e_picked_scales[E_ROW:P, span(c)]),
+            )
             for t in range(PACK):
-                for i, (mw, ms) in enumerate(((xw[c], xs[X_ROW:P, cols(c)]), (ew[c], es[E_ROW:P, cols(c)]))):
+                for i, (w_codes, w_scales, codes, scales) in enumerate(products):
                     nc.tensor.matmul_mx(
                         out=pre[:, t, :],
-                        lhsT=w_codes[i][:, cols(t)].bitcast(FP8X4),
-                        lhsT_scale=w_scales[i][:, cols(t)],
-                        rhs=mw.bitcast(FP8X4),
-                        rhs_scale=ms,
+                        lhsT=w_codes[:, span(t, P)].bitcast(FP8X4),
+                        lhsT_scale=w_scales[:, span(t, P)],
+                        rhs=codes.bitcast(FP8X4),
+                        rhs_scale=scales,
                         start=(i == 0),
-                        stop=(i == 1),
+                        stop=(i == len(products) - 1),
                     )
-            st[c]["pre"] = pre
+            made["pre", c] = pre
 
-        def gb(c):
-            if H_CAST[c] == "S":
-                st[c]["h_bf"] = sb([P, CH * PACK], BF16, "h_bf%d" % c)
+        def gather_x_rest(c):
+            x_picked.extend(gather_words(x_word_table, offs_sb, c, CHUNKS - c, "x_picked2", after="e_picked0"))
+
+        def gelu(c):
+            nc.scalar.activation(chunk_tile("h", c, F32)[:], made["pre", c][:], ACT.Gelu_apprx_tanh)
+
+        def round_h(c):
+            h_rounded = chunk_tile("h_rounded", c, BF16)
+            if c in H_ROUNDED_ON_VECTOR:
+                round_and_interleave(True, h_rounded, made["h", c])
+            else:
                 nc.scalar.activation(
-                    st[c]["h_bf"][:].rearrange("p (n t) -> p n t", t=PACK),
-                    st[c]["pre"][:].rearrange("p t n -> p n t"),
+                    h_rounded[:].rearrange("p (j t) -> p j t", t=PACK),
+                    made["pre", c][:].rearrange("p t j -> p j t"),
                     ACT.Gelu_apprx_tanh,
                 )
-            else:
-                st[c]["h_bf"] = sb([P, CH * PACK], BF16, "h_bf%d" % c)
-                interleave("V", st[c]["h_bf"], st[c]["h"])
 
-        def gf(c):
-            st[c]["h"] = sb([P, PACK, CH], F32, "h%d" % c)
-            nc.scalar.activation(st[c]["h"][:], st[c]["pre"][:], ACT.Gelu_apprx_tanh)
-
-        def qh(c):
-            hc = sb([P, CH], U32, "h_codes%d" % c)
-            hs = sb([P, CH], U8, "h_scales%d" % c)
-            nc.vector.quantize_mx(out=hc[:].bitcast(FP8X4), scales=hs[:], in_=st[c]["h_bf"][:])
-            z = psum.tile([P, PACK, CH], F32, name="z%d" % c, tag="z%d" % c)
+        def gate(c):
+            h_codes = sbuf([P, CHUNK], U32, "h_codes%d" % c)
+            h_scales = sbuf([P, CHUNK], U8, "h_scales%d" % c)
+            nc.vector.quantize_mx(out=h_codes[:].bitcast(FP8X4), scales=h_scales[:], in_=made["h_rounded", c][:])
+            z = psum.tile([P, PACK, CHUNK], F32, name="z%d" % c, tag="z%d" % c)
             for t in range(PACK):
                 nc.tensor.matmul_mx(
                     out=z[:, t, :],
-                    lhsT=w3w[:, cols(t)].bitcast(FP8X4),
-                    lhsT_scale=w3s[W3_ROW:P, cols(t)],
-                    rhs=hc[:].bitcast(FP8X4),
-                    rhs_scale=hs[:],
+                    lhsT=w3_codes[:, span(t, P)].bitcast(FP8X4),
+                    lhsT_scale=w3_dealt_scales[W3_ROW:P, span(t, P)],
+                    rhs=h_codes[:].bitcast(FP8X4),
+                    rhs_scale=h_scales[:],
                     start=True,
                     stop=True,
                 )
-            st[c]["z"] = z
+            made["z", c] = z
 
-        def th(c):
-            st[c]["th"] = sb([P, PACK, CH], F32, "th%d" % c)
-            nc.scalar.activation(st[c]["th"][:], st[c]["z"][:], ACT.Tanh, scale=0.5)
+        def tanh(c):
+            nc.scalar.activation(chunk_tile("tanh", c, F32)[:], made["z", c][:], ACT.Tanh, scale=0.5)
 
-        def dd(c):
-            st[c]["d"] = sb([P, PACK, CH], F32, "d%d" % c)
-            nc.vector.tensor_tensor(st[c]["d"][:], st[c]["h"][:], skip_sb[c], ALU.subtract)
+        def diff(c):
+            nc.vector.tensor_tensor(chunk_tile("diff", c, F32)[:], made["h", c][:], skip_sb[c], ALU.subtract)
 
-        def mm(c):
-            st[c]["m"] = sb([P, PACK, CH], F32, "m%d" % c)
-            nc.vector.scalar_tensor_tensor(st[c]["m"][:], st[c]["th"][:], 1.0, st[c]["d"][:], ALU.add, ALU.mult)
-
-        def oo(c):
-            st[c]["o"] = sb([P, PACK, CH], F32, "o%d" % c)
-            nc.vector.scalar_tensor_tensor(st[c]["o"][:], st[c]["m"][:], 0.5, skip_sb[c], ALU.mult, ALU.add)
-            nc.sync.dma_start(out=out_rows[:, :, cols(c)], in_=st[c]["o"][:])
-
-        def oc(c):
-            st[c]["o_bf"] = sb([P, CH * PACK], BF16, "o_bf%d" % c)
-            interleave(OUT_CAST[c], st[c]["o_bf"], st[c]["o"])
-
-        def qo(c):
-            nc.vector.quantize_mx(
-                out=out_codes[:, cols(c)].bitcast(FP8X4), scales=out_scales[:, cols(c)], in_=st[c]["o_bf"][:]
+        def scale(c):
+            nc.vector.scalar_tensor_tensor(
+                chunk_tile("scaled", c, F32)[:], made["tanh", c][:], 1.0, made["diff", c][:], ALU.add, ALU.mult
             )
 
-        steps = dict(mm1=mm1, gb=gb, gf=gf, qh=qh, th=th, dd=dd, mm=mm, oo=oo, oc=oc, qo=qo)
-        for item in ORDER.split():
-            steps[item[:-1]](int(item[-1]))
-            if item == "qo2":
-                nc.sync.dma_start(out=words_view(out_1)[:, 0 : 3 * CH], in_=out_codes[:, 0 : 3 * CH].bitcast(I32))
-        nc.sync.dma_start(out=words_view(out_1)[:, 3 * CH : S], in_=out_codes[:, 3 * CH : S].bitcast(I32))
+        def result(c):
+            out = chunk_tile("out", c, F32)
+            nc.vector.scalar_tensor_tensor(out[:], made["scaled", c][:], 0.5, skip_sb[c], ALU.mult, ALU.add)
+            nc.sync.dma_start(out=out_rows[:, :, span(c)], in_=out[:])
+
+        def round_out(c):
+            round_and_interleave(c in OUT_ROUNDED_ON_VECTOR, chunk_tile("out_rounded", c, BF16), made["out", c])
+
+        def quantise_out(c):
+            nc.vector.quantize_mx(
+                out=out_codes[:, span(c)].bitcast(FP8X4), scales=out_scales[:, span(c)], in_=made["out_rounded", c][:]
+            )
+            if c >= CHUNKS - 2:
+                columns = slice(0, (c + 1) * CHUNK) if c == CHUNKS - 2 else span(c)
+                nc.sync.dma_start(out=words_view(out_1)[:, columns], in_=out_codes[:, columns].bitcast(I32))
+
+        steps = dict(
+            layer1=layer1,
+            gather_x_rest=gather_x_rest,
+            gelu=gelu,
+            round_h=round_h,
+            gate=gate,
+            tanh=tanh,
+            diff=diff,
+            scale=scale,
+            result=result,
+            round_out=round_out,
+            quantise_out=quantise_out,
+        )
+        for entry in STEPS.split():
+            step, chunk = entry.split(":")
+            steps[step](int(chunk))
+
         for q in range(4):
             queue = nc.scalar if q < 2 else nc.sync
             queue.dma_start(

@@ -21,15 +21,9 @@ FLOPS = 3 * 2 * 512 * HIDDEN * POSITIONS
 
 X_ROW, E_ROW, W3_ROW = 0, 4, 8
 W1_ON_VECTOR, W2_ON_VECTOR = 64, 48
-H_ROUNDED_ON_VECTOR, OUT_ROUNDED_ON_VECTOR = (1,), (3,)
-WARM_UP_PASSES = 2
-STEPS = (
-    "layer1:0 gather_x_rest:2 layer1:1 round_h:0 gelu:0 layer1:2 gate:0 gelu:1 layer1:3 diff:0 gelu:2 round_h:1 "
-    "round_h:2 diff:1 "
-    "tanh:0 gate:1 diff:2 gelu:3 gate:2 scale:0 round_h:3 diff:3 tanh:1 gate:3 tanh:2 result:0 scale:1 round_out:0 "
-    "scale:2 tanh:3 result:1 scale:3 round_out:1 result:2 result:3 round_out:2 quantise_out:0 quantise_out:1 "
-    "round_out:3 quantise_out:2 quantise_out:3"
-)
+H_CHUNK_ON_VECTOR, OUT_CHUNK_ON_VECTOR = 1, CHUNKS - 1
+GATE_LAG, RESULT_LAG = 2, 3
+X_PIECE = 2
 
 
 def tile_picked_zhwy_gelu_po_kernel(
@@ -127,19 +121,7 @@ def tile_picked_zhwy_gelu_po_kernel(
         w2_scales = sbuf([P, HIDDEN], U8, "w2_scales", after="x_scale_table")
         nc.vector.quantize_mx(out=w2_codes[:].bitcast(FP8X4), scales=w2_scales[:], in_=w2_rounded[:])
 
-        warm_bank = psum.tile([P, HIDDEN], F32, name="warm_bank", tag="z%d" % (CHUNKS - 1))
-        for i in range(WARM_UP_PASSES):
-            nc.tensor.matmul_mx(
-                out=warm_bank[:],
-                lhsT=w1_codes[:, 0:P].bitcast(FP8X4),
-                lhsT_scale=w1_scales[:, 0:P],
-                rhs=w2_codes[:].bitcast(FP8X4),
-                rhs_scale=w2_scales[:],
-                start=True,
-                stop=True,
-            )
-
-        x_picked = gather_words(x_word_table, offs_sb, 0, 2, "x_picked0")
+        x_picked = gather_words(x_word_table, offs_sb, 0, X_PIECE, "x_picked0")
         w3_dealt_scales = sbuf([P, HIDDEN], U8, "w3_dealt_scales")
         deal_columns(w3_dealt_scales, w3_scales_raw)
         e_picked = gather_words(e_word_table, tok_sb, 0, 1, "e_picked0")
@@ -177,15 +159,12 @@ def tile_picked_zhwy_gelu_po_kernel(
                     )
             made["pre", c] = pre
 
-        def gather_x_rest(c):
-            x_picked.extend(gather_words(x_word_table, offs_sb, c, CHUNKS - c, "x_picked2", after="e_picked0"))
-
         def gelu(c):
             nc.scalar.activation(chunk_tile("h", c, F32)[:], made["pre", c][:], ACT.Gelu_apprx_tanh)
 
         def round_h(c):
             h_rounded = chunk_tile("h_rounded", c, BF16)
-            if c in H_ROUNDED_ON_VECTOR:
+            if c == H_CHUNK_ON_VECTOR:
                 round_and_interleave(True, h_rounded, made["h", c])
             else:
                 nc.scalar.activation(
@@ -228,7 +207,7 @@ def tile_picked_zhwy_gelu_po_kernel(
             nc.sync.dma_start(out=out_rows[:, :, span(c)], in_=out[:])
 
         def round_out(c):
-            round_and_interleave(c in OUT_ROUNDED_ON_VECTOR, chunk_tile("out_rounded", c, BF16), made["out", c])
+            round_and_interleave(c == OUT_CHUNK_ON_VECTOR, chunk_tile("out_rounded", c, BF16), made["out", c])
 
         def quantise_out(c):
             nc.vector.quantize_mx(
@@ -238,22 +217,19 @@ def tile_picked_zhwy_gelu_po_kernel(
                 columns = slice(0, (c + 1) * CHUNK) if c == CHUNKS - 2 else span(c)
                 nc.sync.dma_start(out=words_view(out_1)[:, columns], in_=out_codes[:, columns].bitcast(I32))
 
-        steps = dict(
-            layer1=layer1,
-            gather_x_rest=gather_x_rest,
-            gelu=gelu,
-            round_h=round_h,
-            gate=gate,
-            tanh=tanh,
-            diff=diff,
-            scale=scale,
-            result=result,
-            round_out=round_out,
-            quantise_out=quantise_out,
-        )
-        for entry in STEPS.split():
-            step, chunk = entry.split(":")
-            steps[step](int(chunk))
+        layer1(0)
+        x_picked.extend(gather_words(x_word_table, offs_sb, X_PIECE, CHUNKS - X_PIECE, "x_picked2", after="e_picked0"))
+        for step in (round_h, gelu, gate, diff):
+            step(0)
+        pipeline = [(step, 0) for step in (layer1, gelu, round_h, diff, gate)]
+        pipeline.extend([(tanh, GATE_LAG), (scale, GATE_LAG), (result, RESULT_LAG)])
+        for tick in range(1, CHUNKS + RESULT_LAG):
+            for step, lag in pipeline:
+                if 0 <= tick - lag < CHUNKS:
+                    step(tick - lag)
+        for c in range(CHUNKS):
+            round_out(c)
+            quantise_out(c)
 
         for q in range(4):
             queue = nc.scalar if q < 2 else nc.sync

@@ -20,7 +20,7 @@ CHUNKS = POSITIONS // CHUNK
 FLOPS = 3 * 2 * 512 * HIDDEN * POSITIONS
 
 X_ROW, E_ROW, W3_ROW = 0, 4, 8
-W1_ON_VECTOR, W2_ON_VECTOR = 64, 48
+W1_ON_VECTOR, W2_ON_VECTOR = 32, 32
 H_CHUNK_ON_VECTOR, OUT_CHUNK_ON_VECTOR = 1, CHUNKS - 1
 GATE_LAG, RESULT_LAG = 2, 3
 X_PIECE = 2
@@ -44,11 +44,11 @@ def tile_picked_zhwy_gelu_po_kernel(
         def words_view(dram):
             return dram[0].rearrange("p c r -> p (c r)").bitcast(I32)
 
-        def load_scales(clear_on, tile, dram, row):
+        def load_scales(clear_on, queue, tile, dram, row):
             clear_on.memset(tile[:].bitcast(I32), 0)
             rows = dram[0].rearrange("(q r) c -> r q c", r=4)
             for r in range(4):
-                nc.sync.dma_start(out=tile[row + r : P : 32, :].bitcast(I32), in_=rows[r].bitcast(I32))
+                queue.dma_start(out=tile[row + r : P : 32, :].bitcast(I32), in_=rows[r].bitcast(I32))
 
         def load_weight(tile, w):
             nc.sync.dma_start(out=tile[:], in_=w.rearrange("(p j) c -> p j c", j=PACK))
@@ -80,24 +80,24 @@ def tile_picked_zhwy_gelu_po_kernel(
             else:
                 nc.scalar.copy(out=dst_view, in_=src_view)
 
-        w1_raw = sbuf([P, PACK, HIDDEN], F32, "w1_raw")
-        load_weight(w1_raw, w1)
-        offs_sb = lists.tile([P, POSITIONS // 16], U16, name="offs_sb")
-        tok_sb = lists.tile([P, POSITIONS // 16], U16, name="tok_sb")
-        nc.sync.dma_start(offs_sb[:], offs)
-        nc.sync.dma_start(tok_sb[:], tok)
-        e_scale_table = sbuf([P, VOCAB], U8, "e_scale_table")
-        load_scales(nc.gpsimd, e_scale_table, e_scales, E_ROW)
         w2_raw = sbuf([P, PACK, HIDDEN], F32, "w2_raw")
         load_weight(w2_raw, w2)
+        offs_sb = lists.tile([P, POSITIONS // 16], U16, name="offs_sb")
+        tok_sb = lists.tile([P, POSITIONS // 16], U16, name="tok_sb")
+        nc.sync.dma_start(tok_sb[:], tok)
+        nc.sync.dma_start(offs_sb[:], offs)
+        e_scale_table = sbuf([P, VOCAB], U8, "e_scale_table")
+        load_scales(nc.vector, nc.sync, e_scale_table, e_scales, E_ROW)
+        w1_raw = sbuf([P, PACK, HIDDEN], F32, "w1_raw")
+        load_weight(w1_raw, w1)
         x_scale_table = sbuf([P, STATES], U8, "x_scale_table")
-        load_scales(nc.vector, x_scale_table, x_scales, X_ROW)
-        x_word_table = sbuf([P, STATES], U32, "x_word_table")
-        nc.sync.dma_start(out=x_word_table[:].bitcast(I32), in_=words_view(x_words))
+        load_scales(nc.vector, nc.sync, x_scale_table, x_scales, X_ROW)
         w3_scales_raw = sbuf([P, HIDDEN], U8, "w3_scales_raw")
-        load_scales(nc.gpsimd, w3_scales_raw, w3_scales, W3_ROW)
+        load_scales(nc.gpsimd, nc.gpsimd, w3_scales_raw, w3_scales, W3_ROW)
         e_word_table = sbuf([P, VOCAB], U32, "e_word_table")
         nc.sync.dma_start(out=e_word_table[:].bitcast(I32), in_=words_view(e_words))
+        x_word_table = sbuf([P, STATES], U32, "x_word_table")
+        nc.sync.dma_start(out=x_word_table[:].bitcast(I32), in_=words_view(x_words))
         w3_words_raw = sbuf([P, HIDDEN], I32, "w3_words_raw")
         nc.sync.dma_start(out=w3_words_raw[:], in_=words_view(w3_words))
         skip_rows = skip.rearrange("(p t) c -> p t c", t=PACK)
@@ -107,27 +107,27 @@ def tile_picked_zhwy_gelu_po_kernel(
             nc.sync.dma_start(out=skip_half[:], in_=skip_rows[:, :, span(half, 2 * CHUNK)])
             skip_sb.extend(skip_half[:, :, span(c)] for c in range(2))
 
-        w1_rounded = round_and_deal_weight(w1_raw, "w1_rounded", W1_ON_VECTOR)
+        w2_rounded = round_and_deal_weight(w2_raw, "w2_rounded", W2_ON_VECTOR)
         e_picked_scales = sbuf([P, POSITIONS], U8, "e_picked_scales")
         nc.vector.tensor_copy(e_picked_scales[:], e_scale_table[:].indirect(tok_sb[:]))
-        w1_codes = sbuf([P, HIDDEN], U32, "w1_codes")
-        w1_scales = sbuf([P, HIDDEN], U8, "w1_scales", after="e_scale_table")
-        nc.vector.quantize_mx(out=w1_codes[:].bitcast(FP8X4), scales=w1_scales[:], in_=w1_rounded[:])
-
-        w2_rounded = round_and_deal_weight(w2_raw, "w2_rounded", W2_ON_VECTOR)
-        x_picked_scales = sbuf([P, POSITIONS], U8, "x_picked_scales")
-        nc.vector.tensor_copy(x_picked_scales[:], x_scale_table[:].indirect(offs_sb[:]))
         w2_codes = sbuf([P, HIDDEN], U32, "w2_codes")
-        w2_scales = sbuf([P, HIDDEN], U8, "w2_scales", after="x_scale_table")
+        w2_scales = sbuf([P, HIDDEN], U8, "w2_scales", after="e_scale_table")
         nc.vector.quantize_mx(out=w2_codes[:].bitcast(FP8X4), scales=w2_scales[:], in_=w2_rounded[:])
 
-        x_picked = gather_words(x_word_table, offs_sb, 0, X_PIECE, "x_picked0")
-        w3_dealt_scales = sbuf([P, HIDDEN], U8, "w3_dealt_scales")
-        deal_columns(w3_dealt_scales, w3_scales_raw)
+        w1_rounded = round_and_deal_weight(w1_raw, "w1_rounded", W1_ON_VECTOR)
+        x_picked_scales = sbuf([P, POSITIONS], U8, "x_picked_scales")
+        nc.vector.tensor_copy(x_picked_scales[:], x_scale_table[:].indirect(offs_sb[:]))
         e_picked = gather_words(e_word_table, tok_sb, 0, 1, "e_picked0")
         e_picked.extend(gather_words(e_word_table, tok_sb, 1, 1, "e_picked1"))
         e_picked.extend(gather_words(e_word_table, tok_sb, 2, 2, "e_picked2"))
-        w3_codes = sbuf([P, HIDDEN], I32, "w3_codes", after="e_word_table")
+        w1_codes = sbuf([P, HIDDEN], U32, "w1_codes", after="e_word_table")
+        w1_scales = sbuf([P, HIDDEN], U8, "w1_scales")
+        nc.vector.quantize_mx(out=w1_codes[:].bitcast(FP8X4), scales=w1_scales[:], in_=w1_rounded[:])
+        w3_dealt_scales = sbuf([P, HIDDEN], U8, "w3_dealt_scales", after="w1_rounded")
+        deal_columns(w3_dealt_scales, w3_scales_raw)
+        x_picked = gather_words(x_word_table, offs_sb, 0, X_PIECE, "x_picked0")
+        x_picked.extend(gather_words(x_word_table, offs_sb, X_PIECE, CHUNKS - X_PIECE, "x_picked2"))
+        w3_codes = sbuf([P, HIDDEN], I32, "w3_codes")
         deal_columns(w3_codes, w3_words_raw)
 
         out_rows = out_0.rearrange("(p t) c -> p t c", t=PACK)
@@ -140,24 +140,24 @@ def tile_picked_zhwy_gelu_po_kernel(
             made[what, c] = sbuf(shape, dtype, "%s%d" % (what, c))
             return made[what, c]
 
-        def layer1(c):
-            pre = psum.tile([P, PACK, CHUNK], F32, name="pre%d" % c)
-            products = (
-                (w1_codes, w1_scales, x_picked[c], x_picked_scales[X_ROW:P, span(c)]),
-                (w2_codes, w2_scales, e_picked[c], e_picked_scales[E_ROW:P, span(c)]),
-            )
+        def first_layer_passes(c, w_codes, w_scales, codes, scales, opens):
             for t in range(PACK):
-                for i, (w_codes, w_scales, codes, scales) in enumerate(products):
-                    nc.tensor.matmul_mx(
-                        out=pre[:, t, :],
-                        lhsT=w_codes[:, span(t, P)].bitcast(FP8X4),
-                        lhsT_scale=w_scales[:, span(t, P)],
-                        rhs=codes.bitcast(FP8X4),
-                        rhs_scale=scales,
-                        start=(i == 0),
-                        stop=(i == len(products) - 1),
-                    )
-            made["pre", c] = pre
+                nc.tensor.matmul_mx(
+                    out=made["pre", c][:, t, :],
+                    lhsT=w_codes[:, span(t, P)].bitcast(FP8X4),
+                    lhsT_scale=w_scales[:, span(t, P)],
+                    rhs=codes.bitcast(FP8X4),
+                    rhs_scale=scales,
+                    start=(opens and t == 0),
+                    stop=(not opens and t == PACK - 1),
+                )
+
+        def open_layer1(c):
+            made["pre", c] = psum.tile([P, PACK, CHUNK], F32, name="pre%d" % c)
+            first_layer_passes(c, w2_codes, w2_scales, e_picked[c], e_picked_scales[E_ROW:P, span(c)], True)
+
+        def layer1(c):
+            first_layer_passes(c, w1_codes, w1_scales, x_picked[c], x_picked_scales[X_ROW:P, span(c)], False)
 
         def gelu(c):
             nc.scalar.activation(chunk_tile("h", c, F32)[:], made["pre", c][:], ACT.Gelu_apprx_tanh)
@@ -217,8 +217,9 @@ def tile_picked_zhwy_gelu_po_kernel(
                 columns = slice(0, (c + 1) * CHUNK) if c == CHUNKS - 2 else span(c)
                 nc.sync.dma_start(out=words_view(out_1)[:, columns], in_=out_codes[:, columns].bitcast(I32))
 
+        for c in range(CHUNKS):
+            open_layer1(c)
         layer1(0)
-        x_picked.extend(gather_words(x_word_table, offs_sb, X_PIECE, CHUNKS - X_PIECE, "x_picked2", after="e_picked0"))
         for step in (round_h, gelu, gate, diff):
             step(0)
         pipeline = [(step, 0) for step in (layer1, gelu, round_h, diff, gate)]

@@ -55,8 +55,8 @@ def tile_picked_zhwy_gelu_po_kernel(
 
         def round_and_deal_weight(raw, name, on_vector):
             rounded = sbuf([P, HIDDEN * PACK], BF16, name)
-            src = raw[:].rearrange("p j (m t) -> p m t j", t=PACK)
-            dst = rounded[:].rearrange("p (t m j) -> p m t j", t=PACK, j=PACK)
+            src = raw[:].rearrange("p j (m t) -> p m j t", t=PACK)
+            dst = rounded[:].rearrange("p (t m j) -> p m j t", t=PACK, j=PACK)
             nc.vector.tensor_copy(out=dst[:, 0:on_vector], in_=src[:, 0:on_vector])
             nc.scalar.copy(out=dst[:, on_vector:P], in_=src[:, on_vector:P])
             return rounded

@@ -21,9 +21,10 @@ FLOPS = 3 * 2 * 512 * HIDDEN * POSITIONS
 
 X_ROW, E_ROW, W3_ROW = 0, 4, 8
 W1_ON_VECTOR, W2_ON_VECTOR = 32, 32
-H_CHUNK_ON_VECTOR, OUT_CHUNK_ON_VECTOR = 1, CHUNKS - 1
+H_CHUNK_ON_VECTOR, OUT_CHUNK_ON_VECTOR = 0, CHUNKS - 1
 GATE_LAG, RESULT_LAG = 2, 3
 X_PIECE = 2
+SKIP_PIECES = (1, 1, 2)
 
 
 def tile_picked_zhwy_gelu_po_kernel(
@@ -44,11 +45,13 @@ def tile_picked_zhwy_gelu_po_kernel(
         def words_view(dram):
             return dram[0].rearrange("p c r -> p (c r)").bitcast(I32)
 
-        def load_scales(clear_on, queue, tile, dram, row):
+        def load_scales(clear_on, dram, width, row, name):
+            tile = sbuf([P, width], U8, name)
             clear_on.memset(tile[:].bitcast(I32), 0)
             rows = dram[0].rearrange("(q r) c -> r q c", r=4)
             for r in range(4):
-                queue.dma_start(out=tile[row + r : P : 32, :].bitcast(I32), in_=rows[r].bitcast(I32))
+                nc.sync.dma_start(out=tile[row + r : P : 32, :].bitcast(I32), in_=rows[r].bitcast(I32))
+            return tile
 
         def load_weight(tile, w):
             nc.sync.dma_start(out=tile[:], in_=w.rearrange("(p j) c -> p j c", j=PACK))
@@ -80,54 +83,52 @@ def tile_picked_zhwy_gelu_po_kernel(
             else:
                 nc.scalar.copy(out=dst_view, in_=src_view)
 
-        w2_raw = sbuf([P, PACK, HIDDEN], F32, "w2_raw")
-        load_weight(w2_raw, w2)
-        offs_sb = lists.tile([P, POSITIONS // 16], U16, name="offs_sb")
-        tok_sb = lists.tile([P, POSITIONS // 16], U16, name="tok_sb")
-        nc.sync.dma_start(tok_sb[:], tok)
-        nc.sync.dma_start(offs_sb[:], offs)
-        e_scale_table = sbuf([P, VOCAB], U8, "e_scale_table")
-        load_scales(nc.vector, nc.sync, e_scale_table, e_scales, E_ROW)
         w1_raw = sbuf([P, PACK, HIDDEN], F32, "w1_raw")
         load_weight(w1_raw, w1)
-        x_scale_table = sbuf([P, STATES], U8, "x_scale_table")
-        load_scales(nc.vector, nc.sync, x_scale_table, x_scales, X_ROW)
-        w3_scales_raw = sbuf([P, HIDDEN], U8, "w3_scales_raw")
-        load_scales(nc.gpsimd, nc.gpsimd, w3_scales_raw, w3_scales, W3_ROW)
-        e_word_table = sbuf([P, VOCAB], U32, "e_word_table")
-        nc.sync.dma_start(out=e_word_table[:].bitcast(I32), in_=words_view(e_words))
+        offs_sb = lists.tile([P, POSITIONS // 16], U16, name="offs_sb")
+        tok_sb = lists.tile([P, POSITIONS // 16], U16, name="tok_sb")
+        nc.sync.dma_start(offs_sb[:], offs)
+        nc.sync.dma_start(tok_sb[:], tok)
+        e_scale_table = load_scales(nc.gpsimd, e_scales, VOCAB, E_ROW, "e_scale_table")
+        w2_raw = sbuf([P, PACK, HIDDEN], F32, "w2_raw")
+        load_weight(w2_raw, w2)
+        x_scale_table = load_scales(nc.vector, x_scales, STATES, X_ROW, "x_scale_table")
         x_word_table = sbuf([P, STATES], U32, "x_word_table")
         nc.sync.dma_start(out=x_word_table[:].bitcast(I32), in_=words_view(x_words))
+        w3_scales_raw = load_scales(nc.gpsimd, w3_scales, HIDDEN, W3_ROW, "w3_scales_raw")
+        e_word_table = sbuf([P, VOCAB], U32, "e_word_table")
+        nc.sync.dma_start(out=e_word_table[:].bitcast(I32), in_=words_view(e_words))
         w3_words_raw = sbuf([P, HIDDEN], I32, "w3_words_raw")
         nc.sync.dma_start(out=w3_words_raw[:], in_=words_view(w3_words))
         skip_rows = skip.rearrange("(p t) c -> p t c", t=PACK)
         skip_sb = []
-        for half in range(2):
-            skip_half = sbuf([P, PACK, 2 * CHUNK], F32, "skip_half%d" % half)
-            nc.sync.dma_start(out=skip_half[:], in_=skip_rows[:, :, span(half, 2 * CHUNK)])
-            skip_sb.extend(skip_half[:, :, span(c)] for c in range(2))
-
-        w2_rounded = round_and_deal_weight(w2_raw, "w2_rounded", W2_ON_VECTOR)
-        e_picked_scales = sbuf([P, POSITIONS], U8, "e_picked_scales")
-        nc.vector.tensor_copy(e_picked_scales[:], e_scale_table[:].indirect(tok_sb[:]))
-        w2_codes = sbuf([P, HIDDEN], U32, "w2_codes")
-        w2_scales = sbuf([P, HIDDEN], U8, "w2_scales", after="e_scale_table")
-        nc.vector.quantize_mx(out=w2_codes[:].bitcast(FP8X4), scales=w2_scales[:], in_=w2_rounded[:])
+        for chunks in SKIP_PIECES:
+            first = len(skip_sb)
+            piece = sbuf([P, PACK, chunks * CHUNK], F32, "skip%d" % first)
+            nc.sync.dma_start(out=piece[:], in_=skip_rows[:, :, first * CHUNK : (first + chunks) * CHUNK])
+            skip_sb.extend(piece[:, :, span(c)] for c in range(chunks))
 
         w1_rounded = round_and_deal_weight(w1_raw, "w1_rounded", W1_ON_VECTOR)
+        e_picked_scales = sbuf([P, POSITIONS], U8, "e_picked_scales")
+        nc.vector.tensor_copy(e_picked_scales[:], e_scale_table[:].indirect(tok_sb[:]))
+        w1_codes = sbuf([P, HIDDEN], U32, "w1_codes")
+        w1_scales = sbuf([P, HIDDEN], U8, "w1_scales", after="e_scale_table")
+        nc.vector.quantize_mx(out=w1_codes[:].bitcast(FP8X4), scales=w1_scales[:], in_=w1_rounded[:])
+
+        w2_rounded = round_and_deal_weight(w2_raw, "w2_rounded", W2_ON_VECTOR)
         x_picked_scales = sbuf([P, POSITIONS], U8, "x_picked_scales")
         nc.vector.tensor_copy(x_picked_scales[:], x_scale_table[:].indirect(offs_sb[:]))
+        w2_codes = sbuf([P, HIDDEN], U32, "w2_codes")
+        w2_scales = sbuf([P, HIDDEN], U8, "w2_scales", after="x_scale_table")
+        nc.vector.quantize_mx(out=w2_codes[:].bitcast(FP8X4), scales=w2_scales[:], in_=w2_rounded[:])
+
+        x_picked = gather_words(x_word_table, offs_sb, 0, X_PIECE, "x_picked0")
+        w3_dealt_scales = sbuf([P, HIDDEN], U8, "w3_dealt_scales")
+        deal_columns(w3_dealt_scales, w3_scales_raw)
         e_picked = gather_words(e_word_table, tok_sb, 0, 1, "e_picked0")
         e_picked.extend(gather_words(e_word_table, tok_sb, 1, 1, "e_picked1"))
         e_picked.extend(gather_words(e_word_table, tok_sb, 2, 2, "e_picked2"))
-        w1_codes = sbuf([P, HIDDEN], U32, "w1_codes", after="e_word_table")
-        w1_scales = sbuf([P, HIDDEN], U8, "w1_scales")
-        nc.vector.quantize_mx(out=w1_codes[:].bitcast(FP8X4), scales=w1_scales[:], in_=w1_rounded[:])
-        w3_dealt_scales = sbuf([P, HIDDEN], U8, "w3_dealt_scales", after="w1_rounded")
-        deal_columns(w3_dealt_scales, w3_scales_raw)
-        x_picked = gather_words(x_word_table, offs_sb, 0, X_PIECE, "x_picked0")
-        x_picked.extend(gather_words(x_word_table, offs_sb, X_PIECE, CHUNKS - X_PIECE, "x_picked2"))
-        w3_codes = sbuf([P, HIDDEN], I32, "w3_codes")
+        w3_codes = sbuf([P, HIDDEN], I32, "w3_codes", after="e_word_table")
         deal_columns(w3_codes, w3_words_raw)
 
         out_rows = out_0.rearrange("(p t) c -> p t c", t=PACK)
@@ -154,10 +155,12 @@ def tile_picked_zhwy_gelu_po_kernel(
 
         def open_layer1(c):
             made["pre", c] = psum.tile([P, PACK, CHUNK], F32, name="pre%d" % c)
-            first_layer_passes(c, w2_codes, w2_scales, e_picked[c], e_picked_scales[E_ROW:P, span(c)], True)
+            first_layer_passes(c, w1_codes, w1_scales, x_picked[c], x_picked_scales[X_ROW:P, span(c)], True)
 
         def layer1(c):
-            first_layer_passes(c, w1_codes, w1_scales, x_picked[c], x_picked_scales[X_ROW:P, span(c)], False)
+            if c >= X_PIECE:
+                open_layer1(c)
+            first_layer_passes(c, w2_codes, w2_scales, e_picked[c], e_picked_scales[E_ROW:P, span(c)], False)
 
         def gelu(c):
             nc.scalar.activation(chunk_tile("h", c, F32)[:], made["pre", c][:], ACT.Gelu_apprx_tanh)
@@ -217,14 +220,13 @@ def tile_picked_zhwy_gelu_po_kernel(
                 columns = slice(0, (c + 1) * CHUNK) if c == CHUNKS - 2 else span(c)
                 nc.sync.dma_start(out=words_view(out_1)[:, columns], in_=out_codes[:, columns].bitcast(I32))
 
-        for c in range(CHUNKS):
+        for c in range(X_PIECE):
             open_layer1(c)
         layer1(0)
-        for step in (round_h, gelu, gate, diff):
-            step(0)
-        pipeline = [(step, 0) for step in (layer1, gelu, round_h, diff, gate)]
+        x_picked.extend(gather_words(x_word_table, offs_sb, X_PIECE, CHUNKS - X_PIECE, "x_picked2", after="e_picked0"))
+        pipeline = [(layer1, -1)] + [(step, 0) for step in (gelu, round_h, diff, gate)]
         pipeline.extend([(tanh, GATE_LAG), (scale, GATE_LAG), (result, RESULT_LAG)])
-        for tick in range(1, CHUNKS + RESULT_LAG):
+        for tick in range(CHUNKS + RESULT_LAG):
             for step, lag in pipeline:
                 if 0 <= tick - lag < CHUNKS:
                     step(tick - lag)

@@ -21,9 +21,11 @@ FLOPS = 3 * 2 * 512 * HIDDEN * POSITIONS
 
 X_ROW, E_ROW, W3_ROW = 0, 4, 8
 W1_ON_VECTOR, W2_ON_VECTOR = 32, 32
-H_CHUNK_ON_VECTOR, OUT_CHUNK_ON_VECTOR = 0, CHUNKS - 1
+H_CHUNK_ON_VECTOR = 0
+LAST_ON_SCALAR = 48
 GATE_LAG, RESULT_LAG = 2, 3
 X_PIECE = 2
+WARM_UPS = 3
 SKIP_PIECES = (1, 1, 2)
 
 
@@ -76,8 +78,8 @@ def tile_picked_zhwy_gelu_po_kernel(
             return [picked[:, span(c)] for c in range(chunks)]
 
         def round_and_interleave(on_vector, dst, src):
-            dst_view = dst[:].rearrange("p (c i t) -> p c t i", i=4, t=PACK)
-            src_view = src[:].rearrange("p t (c i) -> p c t i", i=4)
+            dst_view = dst.rearrange("p (c i t) -> p c t i", i=4, t=PACK)
+            src_view = src.rearrange("p t (c i) -> p c t i", i=4)
             if on_vector:
                 nc.vector.tensor_copy(out=dst_view, in_=src_view)
             else:
@@ -128,8 +130,11 @@ def tile_picked_zhwy_gelu_po_kernel(
         e_picked = gather_words(e_word_table, tok_sb, 0, 1, "e_picked0")
         e_picked.extend(gather_words(e_word_table, tok_sb, 1, 1, "e_picked1"))
         e_picked.extend(gather_words(e_word_table, tok_sb, 2, 2, "e_picked2"))
-        w3_codes = sbuf([P, HIDDEN], I32, "w3_codes", after="e_word_table")
-        deal_columns(w3_codes, w3_words_raw)
+        w3_codes = sbuf([P, HIDDEN], I32, "w3_codes")
+        nc.gpsimd.tensor_copy(
+            out=w3_codes[:].rearrange("p (t m) -> p t m", t=PACK),
+            in_=w3_words_raw[:].rearrange("p (m t) -> p t m", t=PACK),
+        )
 
         out_rows = out_0.rearrange("(p t) c -> p t c", t=PACK)
         out_codes = sbuf([P, POSITIONS], U32, "out_codes")
@@ -168,7 +173,7 @@ def tile_picked_zhwy_gelu_po_kernel(
         def round_h(c):
             h_rounded = chunk_tile("h_rounded", c, BF16)
             if c == H_CHUNK_ON_VECTOR:
-                round_and_interleave(True, h_rounded, made["h", c])
+                round_and_interleave(True, h_rounded[:], made["h", c][:])
             else:
                 nc.scalar.activation(
                     h_rounded[:].rearrange("p (j t) -> p j t", t=PACK),
@@ -210,7 +215,11 @@ def tile_picked_zhwy_gelu_po_kernel(
             nc.sync.dma_start(out=out_rows[:, :, span(c)], in_=out[:])
 
         def round_out(c):
-            round_and_interleave(c == OUT_CHUNK_ON_VECTOR, chunk_tile("out_rounded", c, BF16), made["out", c])
+            rounded, out = chunk_tile("out_rounded", c, BF16), made["out", c]
+            on_scalar = LAST_ON_SCALAR if c == CHUNKS - 1 else CHUNK
+            round_and_interleave(False, rounded[:, 0 : on_scalar * PACK], out[:, :, 0:on_scalar])
+            if on_scalar < CHUNK:
+                round_and_interleave(True, rounded[:, on_scalar * PACK : CHUNK * PACK], out[:, :, on_scalar:CHUNK])
 
         def quantise_out(c):
             nc.vector.quantize_mx(
@@ -220,6 +229,17 @@ def tile_picked_zhwy_gelu_po_kernel(
                 columns = slice(0, (c + 1) * CHUNK) if c == CHUNKS - 2 else span(c)
                 nc.sync.dma_start(out=words_view(out_1)[:, columns], in_=out_codes[:, columns].bitcast(I32))
 
+        unread = psum.tile([P, HIDDEN], F32, name="unread", tag="z%d" % (CHUNKS - 1))
+        for t in range(WARM_UPS):
+            nc.tensor.matmul_mx(
+                out=unread[:],
+                lhsT=w1_codes[:, span(t, P)].bitcast(FP8X4),
+                lhsT_scale=w1_scales[:, span(t, P)],
+                rhs=w1_codes[:].bitcast(FP8X4),
+                rhs_scale=x_picked_scales[X_ROW:P, :],
+                start=True,
+                stop=True,
+            )
         for c in range(X_PIECE):
             open_layer1(c)
         layer1(0)

@@ -20,7 +20,7 @@ CHUNKS = POSITIONS // CHUNK
 FLOPS = 3 * 2 * 512 * HIDDEN * POSITIONS
 
 X_ROW, E_ROW, W3_ROW = 0, 4, 8
-W1_ON_VECTOR, W2_ON_VECTOR = 32, 32
+W1_ON_VECTOR, W2_ON_VECTOR = 32, 48
 H_CHUNK_ON_VECTOR = 0
 LAST_ON_SCALAR = 48
 GATE_LAG, RESULT_LAG = 2, 3
@@ -67,8 +67,8 @@ def tile_picked_zhwy_gelu_po_kernel(
             return rounded
 
         def deal_columns(dealt, raw):
-            nc.vector.tensor_copy(
-                out=dealt[:].rearrange("p (t m) -> p m t", t=PACK), in_=raw[:].rearrange("p (m t) -> p m t", t=PACK)
+            nc.gpsimd.tensor_copy(
+                out=dealt[:].rearrange("p (t m) -> p t m", t=PACK), in_=raw[:].rearrange("p (m t) -> p t m", t=PACK)
             )
 
         def gather_words(table, offsets, first_chunk, chunks, name, after=None):
@@ -119,22 +119,21 @@ def tile_picked_zhwy_gelu_po_kernel(
 
         w2_rounded = round_and_deal_weight(w2_raw, "w2_rounded", W2_ON_VECTOR)
         x_picked_scales = sbuf([P, POSITIONS], U8, "x_picked_scales")
-        nc.vector.tensor_copy(x_picked_scales[:], x_scale_table[:].indirect(offs_sb[:]))
+        for half in range(2):
+            columns = span(half, POSITIONS // 32)
+            nc.vector.tensor_copy(x_picked_scales[:, span(half, POSITIONS // 2)], x_scale_table[:].indirect(offs_sb[:, columns]))
         w2_codes = sbuf([P, HIDDEN], U32, "w2_codes")
         w2_scales = sbuf([P, HIDDEN], U8, "w2_scales", after="x_scale_table")
         nc.vector.quantize_mx(out=w2_codes[:].bitcast(FP8X4), scales=w2_scales[:], in_=w2_rounded[:])
 
         x_picked = gather_words(x_word_table, offs_sb, 0, X_PIECE, "x_picked0")
-        w3_dealt_scales = sbuf([P, HIDDEN], U8, "w3_dealt_scales")
+        w3_dealt_scales = sbuf([P, HIDDEN], U8, "w3_dealt_scales", after="w2_rounded")
         deal_columns(w3_dealt_scales, w3_scales_raw)
         e_picked = gather_words(e_word_table, tok_sb, 0, 1, "e_picked0")
         e_picked.extend(gather_words(e_word_table, tok_sb, 1, 1, "e_picked1"))
         e_picked.extend(gather_words(e_word_table, tok_sb, 2, 2, "e_picked2"))
         w3_codes = sbuf([P, HIDDEN], I32, "w3_codes")
-        nc.gpsimd.tensor_copy(
-            out=w3_codes[:].rearrange("p (t m) -> p t m", t=PACK),
-            in_=w3_words_raw[:].rearrange("p (m t) -> p t m", t=PACK),
-        )
+        deal_columns(w3_codes, w3_words_raw)
 
         out_rows = out_0.rearrange("(p t) c -> p t c", t=PACK)
         out_codes = sbuf([P, POSITIONS], U32, "out_codes")
@@ -158,14 +157,13 @@ def tile_picked_zhwy_gelu_po_kernel(
                     stop=(not opens and t == PACK - 1),
                 )
 
-        def open_layer1(c):
-            made["pre", c] = psum.tile([P, PACK, CHUNK], F32, name="pre%d" % c)
-            first_layer_passes(c, w1_codes, w1_scales, x_picked[c], x_picked_scales[X_ROW:P, span(c)], True)
-
         def layer1(c):
-            if c >= X_PIECE:
-                open_layer1(c)
-            first_layer_passes(c, w2_codes, w2_scales, e_picked[c], e_picked_scales[E_ROW:P, span(c)], False)
+            made["pre", c] = psum.tile([P, PACK, CHUNK], F32, name="pre%d" % c)
+            over_x = (w1_codes, w1_scales, x_picked[c], x_picked_scales[X_ROW:P, span(c)])
+            over_e = (w2_codes, w2_scales, e_picked[c], e_picked_scales[E_ROW:P, span(c)])
+            first, second = (over_x, over_e) if c == 0 else (over_e, over_x)
+            first_layer_passes(c, *first, True)
+            first_layer_passes(c, *second, False)
 
         def gelu(c):
             nc.scalar.activation(chunk_tile("h", c, F32)[:], made["pre", c][:], ACT.Gelu_apprx_tanh)
@@ -234,14 +232,12 @@ def tile_picked_zhwy_gelu_po_kernel(
             nc.tensor.matmul_mx(
                 out=unread[:],
                 lhsT=w1_codes[:, span(t, P)].bitcast(FP8X4),
-                lhsT_scale=w1_scales[:, span(t, P)],
+                lhsT_scale=x_picked_scales[X_ROW:P, span(0, P)],
                 rhs=w1_codes[:].bitcast(FP8X4),
-                rhs_scale=x_picked_scales[X_ROW:P, :],
+                rhs_scale=w1_scales[:],
                 start=True,
                 stop=True,
             )
-        for c in range(X_PIECE):
-            open_layer1(c)
         layer1(0)
         x_picked.extend(gather_words(x_word_table, offs_sb, X_PIECE, CHUNKS - X_PIECE, "x_picked2", after="e_picked0"))
         pipeline = [(layer1, -1)] + [(step, 0) for step in (gelu, round_h, diff, gate)]

@@ -223,8 +223,8 @@ def tile_picked_zhwy_gelu_po_kernel(
             nc.vector.quantize_mx(
                 out=out_codes[:, span(c)].bitcast(FP8X4), scales=out_scales[:, span(c)], in_=made["out_rounded", c][:]
             )
-            if c >= CHUNKS - 2:
-                columns = slice(0, (c + 1) * CHUNK) if c == CHUNKS - 2 else span(c)
+            if c % 2 == 1:
+                columns = span(c // 2, 2 * CHUNK)
                 nc.sync.dma_start(out=words_view(out_1)[:, columns], in_=out_codes[:, columns].bitcast(I32))
 
         unread = psum.tile([P, HIDDEN], F32, name="unread", tag="z%d" % (CHUNKS - 1))
@@ -241,7 +241,7 @@ def tile_picked_zhwy_gelu_po_kernel(
         layer1(0)
         x_picked.extend(gather_words(x_word_table, offs_sb, X_PIECE, CHUNKS - X_PIECE, "x_picked2", after="e_picked0"))
         pipeline = [(layer1, -1)] + [(step, 0) for step in (gelu, round_h, diff, gate)]
-        pipeline.extend([(tanh, GATE_LAG), (scale, GATE_LAG), (result, RESULT_LAG)])
+        pipeline.extend([(tanh, GATE_LAG), (result, RESULT_LAG), (scale, GATE_LAG)])
         for tick in range(CHUNKS + RESULT_LAG):
             for step, lag in pipeline:
                 if 0 <= tick - lag < CHUNKS:

@@ -1,6 +1,7 @@
 from contextlib import ExitStack
 
 import concourse.mybir as mybir
+from concourse.masks import make_identity
 
 F32 = mybir.dt.float32
 BF16 = mybir.dt.bfloat16
@@ -19,13 +20,12 @@ CHUNK = 128
 CHUNKS = POSITIONS // CHUNK
 FLOPS = 3 * 2 * 512 * HIDDEN * POSITIONS
 
+
 X_ROW, E_ROW, W3_ROW = 0, 4, 8
-W1_ON_VECTOR, W2_ON_VECTOR = 32, 48
-H_CHUNK_ON_VECTOR = 0
+W1_ON_VECTOR, W2_ON_VECTOR = 48, 32
+H_CHUNK_ON_VECTOR = 1
 LAST_ON_SCALAR = 48
-GATE_LAG, RESULT_LAG = 2, 3
-X_PIECE = 2
-WARM_UPS = 3
+X_PIECES = (1, 1, 2)
 SKIP_PIECES = (1, 1, 2)
 
 
@@ -55,8 +55,15 @@ def tile_picked_zhwy_gelu_po_kernel(
                 nc.sync.dma_start(out=tile[row + r : P : 32, :].bitcast(I32), in_=rows[r].bitcast(I32))
             return tile
 
-        def load_weight(tile, w):
+        def load_weight(w, name):
+            tile = sbuf([P, PACK, HIDDEN], F32, name)
             nc.sync.dma_start(out=tile[:], in_=w.rearrange("(p j) c -> p j c", j=PACK))
+            return tile
+
+        def load_words(dram, width, name):
+            tile = sbuf([P, width], U32, name)
+            nc.sync.dma_start(out=tile[:].bitcast(I32), in_=words_view(dram))
+            return tile
 
         def round_and_deal_weight(raw, name, on_vector):
             rounded = sbuf([P, HIDDEN * PACK], BF16, name)
@@ -66,16 +73,17 @@ def tile_picked_zhwy_gelu_po_kernel(
             nc.scalar.copy(out=dst[:, on_vector:P], in_=src[:, on_vector:P])
             return rounded
 
-        def deal_columns(dealt, raw):
-            nc.gpsimd.tensor_copy(
-                out=dealt[:].rearrange("p (t m) -> p t m", t=PACK), in_=raw[:].rearrange("p (m t) -> p t m", t=PACK)
-            )
+        def quantise_weight(rounded, name, after=None):
+            codes = sbuf([P, HIDDEN], U32, name + "_codes")
+            scales = sbuf([P, HIDDEN], U8, name + "_scales", after)
+            nc.vector.quantize_mx(out=codes[:].bitcast(FP8X4), scales=scales[:], in_=rounded[:])
+            return codes, scales
 
-        def gather_words(table, offsets, first_chunk, chunks, name, after=None):
-            picked = sbuf([P, chunks * CHUNK], U32, name, after)
+        def gather(table, offsets, first_chunk, chunks, dtype, name):
+            picked = sbuf([P, chunks * CHUNK], dtype, name)
             columns = slice(first_chunk * CHUNK // 16, (first_chunk + chunks) * CHUNK // 16)
             nc.vector.tensor_copy(picked[:], table[:].indirect(offsets[:, columns]))
-            return [picked[:, span(c)] for c in range(chunks)]
+            return picked
 
         def round_and_interleave(on_vector, dst, src):
             dst_view = dst.rearrange("p (c i t) -> p c t i", i=4, t=PACK)
@@ -85,23 +93,17 @@ def tile_picked_zhwy_gelu_po_kernel(
             else:
                 nc.scalar.copy(out=dst_view, in_=src_view)
 
-        w1_raw = sbuf([P, PACK, HIDDEN], F32, "w1_raw")
-        load_weight(w1_raw, w1)
         offs_sb = lists.tile([P, POSITIONS // 16], U16, name="offs_sb")
         tok_sb = lists.tile([P, POSITIONS // 16], U16, name="tok_sb")
-        nc.sync.dma_start(offs_sb[:], offs)
+        w2_raw = load_weight(w2, "w2_raw")
         nc.sync.dma_start(tok_sb[:], tok)
         e_scale_table = load_scales(nc.gpsimd, e_scales, VOCAB, E_ROW, "e_scale_table")
-        w2_raw = sbuf([P, PACK, HIDDEN], F32, "w2_raw")
-        load_weight(w2_raw, w2)
+        e_word_table = load_words(e_words, VOCAB, "e_word_table")
+        w1_raw = load_weight(w1, "w1_raw")
+        nc.sync.dma_start(offs_sb[:], offs)
         x_scale_table = load_scales(nc.vector, x_scales, STATES, X_ROW, "x_scale_table")
-        x_word_table = sbuf([P, STATES], U32, "x_word_table")
-        nc.sync.dma_start(out=x_word_table[:].bitcast(I32), in_=words_view(x_words))
-        w3_scales_raw = load_scales(nc.gpsimd, w3_scales, HIDDEN, W3_ROW, "w3_scales_raw")
-        e_word_table = sbuf([P, VOCAB], U32, "e_word_table")
-        nc.sync.dma_start(out=e_word_table[:].bitcast(I32), in_=words_view(e_words))
-        w3_words_raw = sbuf([P, HIDDEN], I32, "w3_words_raw")
-        nc.sync.dma_start(out=w3_words_raw[:], in_=words_view(w3_words))
+        x_word_table = load_words(x_words, STATES, "x_word_table")
+        w3_scale_rows = load_scales(nc.gpsimd, w3_scales, HIDDEN, W3_ROW, "w3_scale_rows")
         skip_rows = skip.rearrange("(p t) c -> p t c", t=PACK)
         skip_sb = []
         for chunks in SKIP_PIECES:
@@ -109,43 +111,16 @@ def tile_picked_zhwy_gelu_po_kernel(
             piece = sbuf([P, PACK, chunks * CHUNK], F32, "skip%d" % first)
             nc.sync.dma_start(out=piece[:], in_=skip_rows[:, :, first * CHUNK : (first + chunks) * CHUNK])
             skip_sb.extend(piece[:, :, span(c)] for c in range(chunks))
+            if first == 0:
+                w3_codes = load_words(w3_words, HIDDEN, "w3_codes")
 
-        w1_rounded = round_and_deal_weight(w1_raw, "w1_rounded", W1_ON_VECTOR)
-        e_picked_scales = sbuf([P, POSITIONS], U8, "e_picked_scales")
-        nc.vector.tensor_copy(e_picked_scales[:], e_scale_table[:].indirect(tok_sb[:]))
-        w1_codes = sbuf([P, HIDDEN], U32, "w1_codes")
-        w1_scales = sbuf([P, HIDDEN], U8, "w1_scales", after="e_scale_table")
-        nc.vector.quantize_mx(out=w1_codes[:].bitcast(FP8X4), scales=w1_scales[:], in_=w1_rounded[:])
+        identity = sbuf([P, P], F32, "identity")
+        make_identity(nc, identity[:])
 
-        w2_rounded = round_and_deal_weight(w2_raw, "w2_rounded", W2_ON_VECTOR)
-        x_picked_scales = sbuf([P, POSITIONS], U8, "x_picked_scales")
-        for half in range(2):
-            columns = span(half, POSITIONS // 32)
-            nc.vector.tensor_copy(x_picked_scales[:, span(half, POSITIONS // 2)], x_scale_table[:].indirect(offs_sb[:, columns]))
-        w2_codes = sbuf([P, HIDDEN], U32, "w2_codes")
-        w2_scales = sbuf([P, HIDDEN], U8, "w2_scales", after="x_scale_table")
-        nc.vector.quantize_mx(out=w2_codes[:].bitcast(FP8X4), scales=w2_scales[:], in_=w2_rounded[:])
-
-        x_picked = gather_words(x_word_table, offs_sb, 0, X_PIECE, "x_picked0")
-        w3_dealt_scales = sbuf([P, HIDDEN], U8, "w3_dealt_scales", after="w2_rounded")
-        deal_columns(w3_dealt_scales, w3_scales_raw)
-        e_picked = gather_words(e_word_table, tok_sb, 0, 1, "e_picked0")
-        e_picked.extend(gather_words(e_word_table, tok_sb, 1, 1, "e_picked1"))
-        e_picked.extend(gather_words(e_word_table, tok_sb, 2, 2, "e_picked2"))
-        w3_codes = sbuf([P, HIDDEN], I32, "w3_codes")
-        deal_columns(w3_codes, w3_words_raw)
-
-        out_rows = out_0.rearrange("(p t) c -> p t c", t=PACK)
-        out_codes = sbuf([P, POSITIONS], U32, "out_codes")
-        out_scales = sbuf([P, POSITIONS], U8, "out_scales")
         made = {}
 
-        def chunk_tile(what, c, dtype):
-            shape = [P, PACK, CHUNK] if dtype == F32 else [P, CHUNK * PACK]
-            made[what, c] = sbuf(shape, dtype, "%s%d" % (what, c))
-            return made[what, c]
-
-        def first_layer_passes(c, w_codes, w_scales, codes, scales, opens):
+        def first_layer_passes(c, weight, codes, scales, opens):
+            w_codes, w_scales = weight
             for t in range(PACK):
                 nc.tensor.matmul_mx(
                     out=made["pre", c][:, t, :],
@@ -157,59 +132,94 @@ def tile_picked_zhwy_gelu_po_kernel(
                     stop=(not opens and t == PACK - 1),
                 )
 
-        def layer1(c):
-            made["pre", c] = psum.tile([P, PACK, CHUNK], F32, name="pre%d" % c)
-            over_x = (w1_codes, w1_scales, x_picked[c], x_picked_scales[X_ROW:P, span(c)])
-            over_e = (w2_codes, w2_scales, e_picked[c], e_picked_scales[E_ROW:P, span(c)])
-            first, second = (over_x, over_e) if c == 0 else (over_e, over_x)
-            first_layer_passes(c, *first, True)
-            first_layer_passes(c, *second, False)
+        w2_rounded = round_and_deal_weight(w2_raw, "w2_rounded", W2_ON_VECTOR)
+        e_picked_scales = gather(e_scale_table, tok_sb, 0, CHUNKS, U8, "e_picked_scales")
+        e_picked = gather(e_word_table, tok_sb, 0, CHUNKS, U32, "e_picked")
+        w2_mx = quantise_weight(w2_rounded, "w2", after="e_word_table")
+        for c in range(CHUNKS):
+            made["pre", c] = psum.tile([P, PACK, CHUNK], F32, name="pre%d" % c, tag="a%d" % c)
+            first_layer_passes(c, w2_mx, e_picked[:, span(c)], e_picked_scales[E_ROW:P, span(c)], True)
+
+        w1_rounded = round_and_deal_weight(w1_raw, "w1_rounded", W1_ON_VECTOR)
+        x_picked_scales = gather(x_scale_table, offs_sb, 0, CHUNKS, U8, "x_picked_scales")
+        w1_mx = quantise_weight(w1_rounded, "w1", after="x_scale_table")
+        first = 0
+        for chunks in X_PIECES:
+            x_picked = gather(x_word_table, offs_sb, first, chunks, U32, "x_picked%d" % first)
+            for c in range(chunks):
+                first_layer_passes(first + c, w1_mx, x_picked[:, span(c)], x_picked_scales[X_ROW:P, span(first + c)], False)
+            first = first + chunks
+
+        out_rows = out_0.rearrange("(p t) c -> p t c", t=PACK)
+        out_codes = sbuf([P, POSITIONS], U32, "out_codes")
+        out_scales = sbuf([P, POSITIONS], U8, "out_scales")
+
+        def chunk_tile(what, c, dtype):
+            shape = [P, PACK, CHUNK] if dtype == F32 else [P, CHUNK * PACK]
+            made[what, c] = sbuf(shape, dtype, "%s%d" % (what, c))
+            return made[what, c]
 
         def gelu(c):
             nc.scalar.activation(chunk_tile("h", c, F32)[:], made["pre", c][:], ACT.Gelu_apprx_tanh)
 
-        def round_h(c):
-            h_rounded = chunk_tile("h_rounded", c, BF16)
-            if c == H_CHUNK_ON_VECTOR:
-                round_and_interleave(True, h_rounded[:], made["h", c][:])
-            else:
+        def round_h_on_scalar(c):
+            if c != H_CHUNK_ON_VECTOR:
                 nc.scalar.activation(
-                    h_rounded[:].rearrange("p (j t) -> p j t", t=PACK),
+                    chunk_tile("h_rounded", c, BF16)[:].rearrange("p (j t) -> p j t", t=PACK),
                     made["pre", c][:].rearrange("p t j -> p j t"),
                     ACT.Gelu_apprx_tanh,
                 )
+
+        def round_h_on_vector(c):
+            if c == H_CHUNK_ON_VECTOR:
+                round_and_interleave(True, chunk_tile("h_rounded", c, BF16)[:], made["h", c][:])
 
         def gate(c):
             h_codes = sbuf([P, CHUNK], U32, "h_codes%d" % c)
             h_scales = sbuf([P, CHUNK], U8, "h_scales%d" % c)
             nc.vector.quantize_mx(out=h_codes[:].bitcast(FP8X4), scales=h_scales[:], in_=made["h_rounded", c][:])
-            z = psum.tile([P, PACK, CHUNK], F32, name="z%d" % c, tag="z%d" % c)
-            for t in range(PACK):
-                nc.tensor.matmul_mx(
-                    out=z[:, t, :],
-                    lhsT=w3_codes[:, span(t, P)].bitcast(FP8X4),
-                    lhsT_scale=w3_dealt_scales[W3_ROW:P, span(t, P)],
-                    rhs=h_codes[:].bitcast(FP8X4),
-                    rhs_scale=h_scales[:],
-                    start=True,
-                    stop=True,
-                )
+            z = psum.tile([P, HIDDEN], F32, name="z%d" % c, tag="a%d" % c)
+            nc.tensor.matmul_mx(
+                out=z[:],
+                lhsT=h_codes[:].bitcast(FP8X4),
+                lhsT_scale=h_scales[:],
+                rhs=w3_codes[:].bitcast(FP8X4),
+                rhs_scale=w3_scale_rows[W3_ROW:P, :],
+                start=True,
+                stop=True,
+            )
             made["z", c] = z
 
-        def tanh(c):
-            nc.scalar.activation(chunk_tile("tanh", c, F32)[:], made["z", c][:], ACT.Tanh, scale=0.5)
+        def turn(out, src, start, stop):
+            nc.tensor.matmul(out, lhsT=src, rhs=identity[:], is_transpose=True, start=start, stop=stop)
 
         def diff(c):
-            nc.vector.tensor_tensor(chunk_tile("diff", c, F32)[:], made["h", c][:], skip_sb[c], ALU.subtract)
+            negated = chunk_tile("negated", c, F32)
+            nc.gpsimd.tensor_scalar(
+                out=negated[:], in0=skip_sb[c], scalar1=-1.0, scalar2=0.0, op0=ALU.mult, op1=ALU.add
+            )
+            d = psum.tile([P, PACK, P], F32, name="d%d" % c, tag="b%d" % c)
+            for t in range(PACK):
+                turn(d[:, t, :], negated[:, t, :], True, False)
+                turn(d[:, t, :], made["h", c][:, t, :], False, True)
+            made["d", c] = d
+
+        def tanh(c):
+            nc.scalar.activation(
+                chunk_tile("tanh", c, F32)[:], made["z", c][:].rearrange("j (p t) -> j t p", t=PACK), ACT.Tanh, scale=0.5
+            )
 
         def scale(c):
-            nc.vector.scalar_tensor_tensor(
-                chunk_tile("scaled", c, F32)[:], made["tanh", c][:], 1.0, made["diff", c][:], ALU.add, ALU.mult
-            )
+            scaled = chunk_tile("scaled", c, F32)
+            nc.vector.scalar_tensor_tensor(scaled[:], made["tanh", c][:], 1.0, made["d", c][:], ALU.add, ALU.mult)
+            back = psum.tile([P, PACK, CHUNK], F32, name="back%d" % c, tag="b%d" % c)
+            for t in range(PACK):
+                turn(back[:, t, :], scaled[:, t, :], True, True)
+            made["back", c] = back
 
         def result(c):
             out = chunk_tile("out", c, F32)
-            nc.vector.scalar_tensor_tensor(out[:], made["scaled", c][:], 0.5, skip_sb[c], ALU.mult, ALU.add)
+            nc.vector.scalar_tensor_tensor(out[:], made["back", c][:], 0.5, skip_sb[c], ALU.mult, ALU.add)
             nc.sync.dma_start(out=out_rows[:, :, span(c)], in_=out[:])
 
         def round_out(c):
@@ -227,22 +237,9 @@ def tile_picked_zhwy_gelu_po_kernel(
                 columns = span(c // 2, 2 * CHUNK)
                 nc.sync.dma_start(out=words_view(out_1)[:, columns], in_=out_codes[:, columns].bitcast(I32))
 
-        unread = psum.tile([P, HIDDEN], F32, name="unread", tag="z%d" % (CHUNKS - 1))
-        for t in range(WARM_UPS):
-            nc.tensor.matmul_mx(
-                out=unread[:],
-                lhsT=w1_codes[:, span(t, P)].bitcast(FP8X4),
-                lhsT_scale=x_picked_scales[X_ROW:P, span(0, P)],
-                rhs=w1_codes[:].bitcast(FP8X4),
-                rhs_scale=w1_scales[:],
-                start=True,
-                stop=True,
-            )
-        layer1(0)
-        x_picked.extend(gather_words(x_word_table, offs_sb, X_PIECE, CHUNKS - X_PIECE, "x_picked2", after="e_picked0"))
-        pipeline = [(layer1, -1)] + [(step, 0) for step in (gelu, round_h, diff, gate)]
-        pipeline.extend([(tanh, GATE_LAG), (result, RESULT_LAG), (scale, GATE_LAG)])
-        for tick in range(CHUNKS + RESULT_LAG):
+        pipeline = [(step, 0) for step in (round_h_on_scalar, gelu, round_h_on_vector, gate, diff)]
+        pipeline.extend([(tanh, 1), (scale, 1), (result, 2)])
+        for tick in range(CHUNKS + 2):
             for step, lag in pipeline:
                 if 0 <= tick - lag < CHUNKS:
                     step(tick - lag)

@@ -1,7 +1,6 @@
 from contextlib import ExitStack
 
 import concourse.mybir as mybir
-from concourse.masks import make_identity
 
 F32 = mybir.dt.float32
 BF16 = mybir.dt.bfloat16
@@ -22,8 +21,9 @@ FLOPS = 3 * 2 * 512 * HIDDEN * POSITIONS
 
 
 X_ROW, E_ROW, W3_ROW = 0, 4, 8
-W1_ON_VECTOR, W2_ON_VECTOR = 48, 32
-H_CHUNK_ON_VECTOR = 1
+W1_ON_VECTOR, W2_ON_VECTOR = 64, 48
+H_CHUNK_ON_VECTOR = 0
+GATE_LAG, RESULT_LAG = 2, 3
 LAST_ON_SCALAR = 48
 X_PIECES = (1, 1, 2)
 SKIP_PIECES = (1, 1, 2)
@@ -79,6 +79,11 @@ def tile_picked_zhwy_gelu_po_kernel(
             nc.vector.quantize_mx(out=codes[:].bitcast(FP8X4), scales=scales[:], in_=rounded[:])
             return codes, scales
 
+        def deal_columns(dealt, raw):
+            nc.gpsimd.tensor_copy(
+                out=dealt[:].rearrange("p (t m) -> p t m", t=PACK), in_=raw[:].rearrange("p (m t) -> p t m", t=PACK)
+            )
+
         def gather(table, offsets, first_chunk, chunks, dtype, name):
             picked = sbuf([P, chunks * CHUNK], dtype, name)
             columns = slice(first_chunk * CHUNK // 16, (first_chunk + chunks) * CHUNK // 16)
@@ -95,15 +100,16 @@ def tile_picked_zhwy_gelu_po_kernel(
 
         offs_sb = lists.tile([P, POSITIONS // 16], U16, name="offs_sb")
         tok_sb = lists.tile([P, POSITIONS // 16], U16, name="tok_sb")
-        w2_raw = load_weight(w2, "w2_raw")
+        e_word_table = load_words(e_words, VOCAB, "e_word_table")
         nc.sync.dma_start(tok_sb[:], tok)
         e_scale_table = load_scales(nc.gpsimd, e_scales, VOCAB, E_ROW, "e_scale_table")
-        e_word_table = load_words(e_words, VOCAB, "e_word_table")
-        w1_raw = load_weight(w1, "w1_raw")
+        w2_raw = load_weight(w2, "w2_raw")
         nc.sync.dma_start(offs_sb[:], offs)
         x_scale_table = load_scales(nc.vector, x_scales, STATES, X_ROW, "x_scale_table")
-        x_word_table = load_words(x_words, STATES, "x_word_table")
+        w1_raw = load_weight(w1, "w1_raw")
         w3_scale_rows = load_scales(nc.gpsimd, w3_scales, HIDDEN, W3_ROW, "w3_scale_rows")
+        x_word_table = load_words(x_words, STATES, "x_word_table")
+        w3_words_raw = load_words(w3_words, HIDDEN, "w3_words_raw")
         skip_rows = skip.rearrange("(p t) c -> p t c", t=PACK)
         skip_sb = []
         for chunks in SKIP_PIECES:
@@ -111,11 +117,6 @@ def tile_picked_zhwy_gelu_po_kernel(
             piece = sbuf([P, PACK, chunks * CHUNK], F32, "skip%d" % first)
             nc.sync.dma_start(out=piece[:], in_=skip_rows[:, :, first * CHUNK : (first + chunks) * CHUNK])
             skip_sb.extend(piece[:, :, span(c)] for c in range(chunks))
-            if first == 0:
-                w3_codes = load_words(w3_words, HIDDEN, "w3_codes")
-
-        identity = sbuf([P, P], F32, "identity")
-        make_identity(nc, identity[:])
 
         made = {}
 
@@ -132,17 +133,21 @@ def tile_picked_zhwy_gelu_po_kernel(
                     stop=(not opens and t == PACK - 1),
                 )
 
-        w2_rounded = round_and_deal_weight(w2_raw, "w2_rounded", W2_ON_VECTOR)
-        e_picked_scales = gather(e_scale_table, tok_sb, 0, CHUNKS, U8, "e_picked_scales")
         e_picked = gather(e_word_table, tok_sb, 0, CHUNKS, U32, "e_picked")
-        w2_mx = quantise_weight(w2_rounded, "w2", after="e_word_table")
+        e_picked_scales = gather(e_scale_table, tok_sb, 0, CHUNKS, U8, "e_picked_scales")
+        w2_rounded = round_and_deal_weight(w2_raw, "w2_rounded", W2_ON_VECTOR)
+        x_picked_scales = gather(x_scale_table, offs_sb, 0, CHUNKS, U8, "x_picked_scales")
+        w2_mx = quantise_weight(w2_rounded, "w2", after="x_scale_table")
         for c in range(CHUNKS):
-            made["pre", c] = psum.tile([P, PACK, CHUNK], F32, name="pre%d" % c, tag="a%d" % c)
+            made["pre", c] = psum.tile([P, PACK, CHUNK], F32, name="pre%d" % c, tag="pre%d" % c)
             first_layer_passes(c, w2_mx, e_picked[:, span(c)], e_picked_scales[E_ROW:P, span(c)], True)
 
         w1_rounded = round_and_deal_weight(w1_raw, "w1_rounded", W1_ON_VECTOR)
-        x_picked_scales = gather(x_scale_table, offs_sb, 0, CHUNKS, U8, "x_picked_scales")
-        w1_mx = quantise_weight(w1_rounded, "w1", after="x_scale_table")
+        w1_mx = quantise_weight(w1_rounded, "w1")
+        w3_dealt_scales = sbuf([P, HIDDEN], U8, "w3_dealt_scales", after="w1_rounded")
+        deal_columns(w3_dealt_scales, w3_scale_rows)
+        w3_codes = sbuf([P, HIDDEN], U32, "w3_codes")
+        deal_columns(w3_codes, w3_words_raw)
         first = 0
         for chunks in X_PIECES:
             x_picked = gather(x_word_table, offs_sb, first, chunks, U32, "x_picked%d" % first)
@@ -162,64 +167,48 @@ def tile_picked_zhwy_gelu_po_kernel(
         def gelu(c):
             nc.scalar.activation(chunk_tile("h", c, F32)[:], made["pre", c][:], ACT.Gelu_apprx_tanh)
 
-        def round_h_on_scalar(c):
-            if c != H_CHUNK_ON_VECTOR:
+        def round_h(c):
+            h_rounded = chunk_tile("h_rounded", c, BF16)
+            if c == H_CHUNK_ON_VECTOR:
+                round_and_interleave(True, h_rounded[:], made["h", c][:])
+            else:
                 nc.scalar.activation(
-                    chunk_tile("h_rounded", c, BF16)[:].rearrange("p (j t) -> p j t", t=PACK),
+                    h_rounded[:].rearrange("p (j t) -> p j t", t=PACK),
                     made["pre", c][:].rearrange("p t j -> p j t"),
                     ACT.Gelu_apprx_tanh,
                 )
-
-        def round_h_on_vector(c):
-            if c == H_CHUNK_ON_VECTOR:
-                round_and_interleave(True, chunk_tile("h_rounded", c, BF16)[:], made["h", c][:])
 
         def gate(c):
             h_codes = sbuf([P, CHUNK], U32, "h_codes%d" % c)
             h_scales = sbuf([P, CHUNK], U8, "h_scales%d" % c)
             nc.vector.quantize_mx(out=h_codes[:].bitcast(FP8X4), scales=h_scales[:], in_=made["h_rounded", c][:])
-            z = psum.tile([P, HIDDEN], F32, name="z%d" % c, tag="a%d" % c)
-            nc.tensor.matmul_mx(
-                out=z[:],
-                lhsT=h_codes[:].bitcast(FP8X4),
-                lhsT_scale=h_scales[:],
-                rhs=w3_codes[:].bitcast(FP8X4),
-                rhs_scale=w3_scale_rows[W3_ROW:P, :],
-                start=True,
-                stop=True,
-            )
+            z = psum.tile([P, PACK, CHUNK], F32, name="z%d" % c, tag="z%d" % c)
+            for t in range(PACK):
+                nc.tensor.matmul_mx(
+                    out=z[:, t, :],
+                    lhsT=w3_codes[:, span(t, P)].bitcast(FP8X4),
+                    lhsT_scale=w3_dealt_scales[W3_ROW:P, span(t, P)],
+                    rhs=h_codes[:].bitcast(FP8X4),
+                    rhs_scale=h_scales[:],
+                    start=True,
+                    stop=True,
+                )
             made["z", c] = z
 
-        def turn(out, src, start, stop):
-            nc.tensor.matmul(out, lhsT=src, rhs=identity[:], is_transpose=True, start=start, stop=stop)
+        def tanh(c):
+            nc.scalar.activation(chunk_tile("tanh", c, F32)[:], made["z", c][:], ACT.Tanh, scale=0.5)
 
         def diff(c):
-            negated = chunk_tile("negated", c, F32)
-            nc.gpsimd.tensor_scalar(
-                out=negated[:], in0=skip_sb[c], scalar1=-1.0, scalar2=0.0, op0=ALU.mult, op1=ALU.add
-            )
-            d = psum.tile([P, PACK, P], F32, name="d%d" % c, tag="b%d" % c)
-            for t in range(PACK):
-                turn(d[:, t, :], negated[:, t, :], True, False)
-                turn(d[:, t, :], made["h", c][:, t, :], False, True)
-            made["d", c] = d
-
-        def tanh(c):
-            nc.scalar.activation(
-                chunk_tile("tanh", c, F32)[:], made["z", c][:].rearrange("j (p t) -> j t p", t=PACK), ACT.Tanh, scale=0.5
-            )
+            nc.vector.tensor_tensor(chunk_tile("diff", c, F32)[:], made["h", c][:], skip_sb[c], ALU.subtract)
 
         def scale(c):
-            scaled = chunk_tile("scaled", c, F32)
-            nc.vector.scalar_tensor_tensor(scaled[:], made["tanh", c][:], 1.0, made["d", c][:], ALU.add, ALU.mult)
-            back = psum.tile([P, PACK, CHUNK], F32, name="back%d" % c, tag="b%d" % c)
-            for t in range(PACK):
-                turn(back[:, t, :], scaled[:, t, :], True, True)
-            made["back", c] = back
+            nc.vector.scalar_tensor_tensor(
+                chunk_tile("scaled", c, F32)[:], made["tanh", c][:], 1.0, made["diff", c][:], ALU.add, ALU.mult
+            )
 
         def result(c):
             out = chunk_tile("out", c, F32)
-            nc.vector.scalar_tensor_tensor(out[:], made["back", c][:], 0.5, skip_sb[c], ALU.mult, ALU.add)
+            nc.vector.scalar_tensor_tensor(out[:], made["scaled", c][:], 0.5, skip_sb[c], ALU.mult, ALU.add)
             nc.sync.dma_start(out=out_rows[:, :, span(c)], in_=out[:])
 
         def round_out(c):
@@ -237,9 +226,9 @@ def tile_picked_zhwy_gelu_po_kernel(
                 columns = span(c // 2, 2 * CHUNK)
                 nc.sync.dma_start(out=words_view(out_1)[:, columns], in_=out_codes[:, columns].bitcast(I32))
 
-        pipeline = [(step, 0) for step in (round_h_on_scalar, gelu, round_h_on_vector, gate, diff)]
-        pipeline.extend([(tanh, 1), (scale, 1), (result, 2)])
-        for tick in range(CHUNKS + 2):
+        pipeline = [(step, 0) for step in (gelu, round_h, diff, gate)]
+        pipeline.extend([(tanh, GATE_LAG), (result, RESULT_LAG), (scale, GATE_LAG)])
+        for tick in range(CHUNKS + RESULT_LAG):
             for step, lag in pipeline:
                 if 0 <= tick - lag < CHUNKS:
                     step(tick - lag)

@@ -118,6 +118,10 @@ def tile_picked_zhwy_gelu_po_kernel(
             nc.sync.dma_start(out=piece[:], in_=skip_rows[:, :, first * CHUNK : (first + chunks) * CHUNK])
             skip_sb.extend(piece[:, :, span(c)] for c in range(chunks))
 
+        unread = sbuf([P, 2], F32, "unread")
+        nc.vector.memset(unread[:, 0:1], 0.0)
+        nc.scalar.activation(unread[:, 1:2], unread[:, 0:1], ACT.Gelu_apprx_tanh)
+
         made = {}
 
         def first_layer_passes(c, weight, codes, scales, opens):

@@ -21,8 +21,8 @@ FLOPS = 3 * 2 * 512 * HIDDEN * POSITIONS
 
 
 X_ROW, E_ROW, W3_ROW = 0, 4, 8
-W1_ON_VECTOR, W2_ON_VECTOR = 64, 48
-H_CHUNK_ON_VECTOR = 0
+W1_ON_VECTOR, W2_ON_VECTOR = 72, 56
+H_CHUNKS_ON_VECTOR = 2
 GATE_LAG, RESULT_LAG = 2, 3
 LAST_ON_SCALAR = 48
 X_PIECES = (1, 1, 2)
@@ -173,7 +173,7 @@ def tile_picked_zhwy_gelu_po_kernel(
 
         def round_h(c):
             h_rounded = chunk_tile("h_rounded", c, BF16)
-            if c == H_CHUNK_ON_VECTOR:
+            if c < H_CHUNKS_ON_VECTOR:
                 round_and_interleave(True, h_rounded[:], made["h", c][:])
             else:
                 nc.scalar.activation(

@@ -21,7 +21,7 @@ FLOPS = 3 * 2 * 512 * HIDDEN * POSITIONS
 
 
 X_ROW, E_ROW, W3_ROW = 0, 4, 8
-W1_ON_VECTOR, W2_ON_VECTOR = 72, 56
+W1_ON_VECTOR, W2_ON_VECTOR = 32, 56
 H_CHUNKS_ON_VECTOR = 2
 GATE_LAG, RESULT_LAG = 2, 3
 LAST_ON_SCALAR = 48
@@ -146,8 +146,16 @@ def tile_picked_zhwy_gelu_po_kernel(
             made["pre", c] = psum.tile([P, PACK, CHUNK], F32, name="pre%d" % c, tag="pre%d" % c)
             first_layer_passes(c, w2_mx, e_picked[:, span(c)], e_picked_scales[E_ROW:P, span(c)], True)
 
-        w1_rounded = round_and_deal_weight(w1_raw, "w1_rounded", W1_ON_VECTOR)
-        w1_mx = quantise_weight(w1_rounded, "w1")
+        w1_src = w1_raw[:].rearrange("p j (m t) -> p m j t", t=PACK)
+        w1_halves = [sbuf([P, HIDDEN * 2], BF16, name) for name in ("w1_rounded_first", "w1_rounded")]
+        w1_dst = [half[:].rearrange("p (t m j) -> p m j t", t=2, j=PACK) for half in w1_halves]
+        nc.vector.tensor_copy(out=w1_dst[0], in_=w1_src[:, :, :, 0:2])
+        nc.vector.tensor_copy(out=w1_dst[1][:, 0:W1_ON_VECTOR], in_=w1_src[:, 0:W1_ON_VECTOR, :, 2:4])
+        nc.scalar.copy(out=w1_dst[1][:, W1_ON_VECTOR:P], in_=w1_src[:, W1_ON_VECTOR:P, :, 2:4])
+        w1_mx = sbuf([P, HIDDEN], U32, "w1_codes"), sbuf([P, HIDDEN], U8, "w1_scales")
+        for i, half in enumerate(w1_halves):
+            columns = span(i, 2 * P)
+            nc.vector.quantize_mx(out=w1_mx[0][:, columns].bitcast(FP8X4), scales=w1_mx[1][:, columns], in_=half[:])
         w3_dealt_scales = sbuf([P, HIDDEN], U8, "w3_dealt_scales", after="w1_rounded")
         deal_columns(w3_dealt_scales, w3_scale_rows)
         w3_codes = sbuf([P, HIDDEN], U32, "w3_codes")

@@ -24,7 +24,6 @@ X_ROW, E_ROW, W3_ROW = 0, 4, 8
 W1_ON_VECTOR, W2_ON_VECTOR = 32, 56
 H_CHUNKS_ON_VECTOR = 2
 GATE_LAG, RESULT_LAG = 2, 3
-LAST_ON_SCALAR = 48
 X_PIECES = (1, 1, 2)
 SKIP_PIECES = (1, 1, 2)
 
@@ -159,7 +158,10 @@ def tile_picked_zhwy_gelu_po_kernel(
         w3_dealt_scales = sbuf([P, HIDDEN], U8, "w3_dealt_scales", after="w1_rounded")
         deal_columns(w3_dealt_scales, w3_scale_rows)
         w3_codes = sbuf([P, HIDDEN], U32, "w3_codes")
-        deal_columns(w3_codes, w3_words_raw)
+        w3_src = w3_words_raw[:].rearrange("p (m t) -> p m t", t=PACK)
+        w3_dst = w3_codes[:].rearrange("p (t m) -> p m t", t=PACK)
+        nc.scalar.copy(out=w3_dst[:, :, 0:2], in_=w3_src[:, :, 0:2])
+        nc.gpsimd.tensor_copy(out=w3_dst[:, :, 2:4].rearrange("p m t -> p t m"), in_=w3_src[:, :, 2:4].rearrange("p m t -> p t m"))
         first = 0
         for chunks in X_PIECES:
             x_picked = gather(x_word_table, offs_sb, first, chunks, U32, "x_picked%d" % first)
@@ -168,21 +170,31 @@ def tile_picked_zhwy_gelu_po_kernel(
             first = first + chunks
 
         out_rows = out_0.rearrange("(p t) c -> p t c", t=PACK)
-        out_codes = sbuf([P, POSITIONS], U32, "out_codes")
         out_scales = sbuf([P, POSITIONS], U8, "out_scales")
+
+        out_rounded = [sbuf([P, 2 * CHUNK * PACK], BF16, "out_rounded%d" % i) for i in range(2)]
 
         def chunk_tile(what, c, dtype):
             shape = [P, PACK, CHUNK] if dtype == F32 else [P, CHUNK * PACK]
             made[what, c] = sbuf(shape, dtype, "%s%d" % (what, c))
             return made[what, c]
 
+        def parts(c, halved=0):
+            cut = CHUNK // 2
+            return [slice(0, cut), slice(cut, CHUNK)] if c == halved else [slice(0, CHUNK)]
+
         def gelu(c):
-            nc.scalar.activation(chunk_tile("h", c, F32)[:], made["pre", c][:], ACT.Gelu_apprx_tanh)
+            h = chunk_tile("h", c, F32)
+            for part in parts(c):
+                nc.scalar.activation(h[:, :, part], made["pre", c][:, :, part], ACT.Gelu_apprx_tanh)
 
         def round_h(c):
             h_rounded = chunk_tile("h_rounded", c, BF16)
             if c < H_CHUNKS_ON_VECTOR:
-                round_and_interleave(True, h_rounded[:], made["h", c][:])
+                difference = chunk_tile("diff", c, F32)
+                for part in parts(c):
+                    round_and_interleave(True, h_rounded[:, part.start * PACK : part.stop * PACK], made["h", c][:, :, part])
+                    nc.vector.tensor_tensor(difference[:, :, part], made["h", c][:, :, part], skip_sb[c][:, :, part], ALU.subtract)
             else:
                 nc.scalar.activation(
                     h_rounded[:].rearrange("p (j t) -> p j t", t=PACK),
@@ -211,31 +223,40 @@ def tile_picked_zhwy_gelu_po_kernel(
             nc.scalar.activation(chunk_tile("tanh", c, F32)[:], made["z", c][:], ACT.Tanh, scale=0.5)
 
         def diff(c):
-            nc.vector.tensor_tensor(chunk_tile("diff", c, F32)[:], made["h", c][:], skip_sb[c], ALU.subtract)
+            if c >= H_CHUNKS_ON_VECTOR:
+                nc.vector.tensor_tensor(chunk_tile("diff", c, F32)[:], made["h", c][:], skip_sb[c], ALU.subtract)
 
         def scale(c):
-            nc.vector.scalar_tensor_tensor(
-                chunk_tile("scaled", c, F32)[:], made["tanh", c][:], 1.0, made["diff", c][:], ALU.add, ALU.mult
-            )
+            for part in parts(c, CHUNKS - 1):
+                scaled = sbuf([P, PACK, part.stop - part.start], F32, "scaled%d_%d" % (c, part.start))
+                made["scaled", c, part.start] = scaled
+                nc.vector.scalar_tensor_tensor(
+                    scaled[:], made["tanh", c][:, :, part], 1.0, made["diff", c][:, :, part], ALU.add, ALU.mult
+                )
 
         def result(c):
             out = chunk_tile("out", c, F32)
-            nc.vector.scalar_tensor_tensor(out[:], made["scaled", c][:], 0.5, skip_sb[c], ALU.mult, ALU.add)
+            for part in parts(c, CHUNKS - 1):
+                nc.vector.scalar_tensor_tensor(
+                    out[:, :, part], made["scaled", c, part.start][:], 0.5, skip_sb[c][:, :, part], ALU.mult, ALU.add
+                )
             nc.sync.dma_start(out=out_rows[:, :, span(c)], in_=out[:])
 
         def round_out(c):
-            rounded, out = chunk_tile("out_rounded", c, BF16), made["out", c]
-            on_scalar = LAST_ON_SCALAR if c == CHUNKS - 1 else CHUNK
-            round_and_interleave(False, rounded[:, 0 : on_scalar * PACK], out[:, :, 0:on_scalar])
-            if on_scalar < CHUNK:
-                round_and_interleave(True, rounded[:, on_scalar * PACK : CHUNK * PACK], out[:, :, on_scalar:CHUNK])
+            rounded, out = out_rounded[c // 2][:, span(c % 2, CHUNK * PACK)], made["out", c]
+            for part in parts(c, CHUNKS - 1):
+                round_and_interleave(False, rounded[:, part.start * PACK : part.stop * PACK], out[:, :, part])
 
-        def quantise_out(c):
+        def quantise_out(first, chunks):
+            columns = slice(first * CHUNK, (first + chunks) * CHUNK)
+            start = (first % 2) * CHUNK * PACK
             nc.vector.quantize_mx(
-                out=out_codes[:, span(c)].bitcast(FP8X4), scales=out_scales[:, span(c)], in_=made["out_rounded", c][:]
+                out=out_codes[:, columns].bitcast(FP8X4),
+                scales=out_scales[:, columns],
+                in_=out_rounded[first // 2][:, start : start + chunks * CHUNK * PACK],
             )
-            if c % 2 == 1:
-                columns = span(c // 2, 2 * CHUNK)
+            if (first + chunks) % 2 == 0:
+                columns = span(first // 2, 2 * CHUNK)
                 nc.sync.dma_start(out=words_view(out_1)[:, columns], in_=out_codes[:, columns].bitcast(I32))
 
         pipeline = [(step, 0) for step in (gelu, round_h, diff, gate)]
@@ -246,7 +267,9 @@ def tile_picked_zhwy_gelu_po_kernel(
                     step(tick - lag)
         for c in range(CHUNKS):
             round_out(c)
-            quantise_out(c)
+        out_codes = sbuf([P, POSITIONS], U32, "out_codes", after="scaled%d_0" % (CHUNKS - 1))
+        for first, chunks in ((0, 2), (2, 1), (3, 1)):
+            quantise_out(first, chunks)
 
         for q in range(4):
             queue = nc.scalar if q < 2 else nc.sync

@@ -25,7 +25,7 @@ W1_ON_VECTOR, W2_ON_VECTOR = 32, 56
 H_CHUNKS_ON_VECTOR = 2
 GATE_LAG, RESULT_LAG = 2, 3
 X_PIECES = (1, 1, 2)
-SKIP_PIECES = (1, 1, 2)
+SKIP_PIECES = (1, 1, 1, 1)
 
 
 def tile_picked_zhwy_gelu_po_kernel(
@@ -255,9 +255,6 @@ def tile_picked_zhwy_gelu_po_kernel(
                 scales=out_scales[:, columns],
                 in_=out_rounded[first // 2][:, start : start + chunks * CHUNK * PACK],
             )
-            if (first + chunks) % 2 == 0:
-                columns = span(first // 2, 2 * CHUNK)
-                nc.sync.dma_start(out=words_view(out_1)[:, columns], in_=out_codes[:, columns].bitcast(I32))
 
         pipeline = [(step, 0) for step in (gelu, round_h, diff, gate)]
         pipeline.extend([(tanh, GATE_LAG), (result, RESULT_LAG), (scale, GATE_LAG)])
@@ -270,6 +267,7 @@ def tile_picked_zhwy_gelu_po_kernel(
         out_codes = sbuf([P, POSITIONS], U32, "out_codes", after="scaled%d_0" % (CHUNKS - 1))
         for first, chunks in ((0, 2), (2, 1), (3, 1)):
             quantise_out(first, chunks)
+        nc.sync.dma_start(out=words_view(out_1), in_=out_codes[:].bitcast(I32))
 
         for q in range(4):
             queue = nc.scalar if q < 2 else nc.sync

@@ -21,9 +21,10 @@ FLOPS = 3 * 2 * 512 * HIDDEN * POSITIONS
 
 
 X_ROW, E_ROW, W3_ROW = 0, 4, 8
-W1_ON_VECTOR, W2_ON_VECTOR = 32, 56
+W1_ON_VECTOR, W2_ON_VECTOR = 32, 0
 H_CHUNKS_ON_VECTOR = 2
 GATE_LAG, RESULT_LAG = 2, 3
+LAST_PARTS = 4
 X_PIECES = (1, 1, 2)
 SKIP_PIECES = (1, 1, 1, 1)
 
@@ -65,17 +66,21 @@ def tile_picked_zhwy_gelu_po_kernel(
             return tile
 
         def round_and_deal_weight(raw, name, on_vector):
-            rounded = sbuf([P, HIDDEN * PACK], BF16, name)
             src = raw[:].rearrange("p j (m t) -> p m j t", t=PACK)
-            dst = rounded[:].rearrange("p (t m j) -> p m j t", t=PACK, j=PACK)
-            nc.vector.tensor_copy(out=dst[:, 0:on_vector], in_=src[:, 0:on_vector])
-            nc.scalar.copy(out=dst[:, on_vector:P], in_=src[:, on_vector:P])
-            return rounded
+            halves = [sbuf([P, HIDDEN * 2], BF16, name + half) for half in ("_rounded_first", "_rounded")]
+            dst = [half[:].rearrange("p (t m j) -> p m j t", t=2, j=PACK) for half in halves]
+            nc.vector.tensor_copy(out=dst[0], in_=src[:, :, :, 0:2])
+            if on_vector:
+                nc.vector.tensor_copy(out=dst[1][:, 0:on_vector], in_=src[:, 0:on_vector, :, 2:4])
+            nc.scalar.copy(out=dst[1][:, on_vector:P], in_=src[:, on_vector:P, :, 2:4])
+            return halves
 
-        def quantise_weight(rounded, name, after=None):
+        def quantise_weight(halves, name, after=None):
             codes = sbuf([P, HIDDEN], U32, name + "_codes")
             scales = sbuf([P, HIDDEN], U8, name + "_scales", after)
-            nc.vector.quantize_mx(out=codes[:].bitcast(FP8X4), scales=scales[:], in_=rounded[:])
+            for i, half in enumerate(halves):
+                columns = span(i, 2 * P)
+                nc.vector.quantize_mx(out=codes[:, columns].bitcast(FP8X4), scales=scales[:, columns], in_=half[:])
             return codes, scales
 
         def deal_columns(dealt, raw):
@@ -138,23 +143,14 @@ def tile_picked_zhwy_gelu_po_kernel(
 
         e_picked = gather(e_word_table, tok_sb, 0, CHUNKS, U32, "e_picked")
         e_picked_scales = gather(e_scale_table, tok_sb, 0, CHUNKS, U8, "e_picked_scales")
-        w2_rounded = round_and_deal_weight(w2_raw, "w2_rounded", W2_ON_VECTOR)
+        w2_rounded = round_and_deal_weight(w2_raw, "w2", W2_ON_VECTOR)
         x_picked_scales = gather(x_scale_table, offs_sb, 0, CHUNKS, U8, "x_picked_scales")
         w2_mx = quantise_weight(w2_rounded, "w2", after="x_scale_table")
         for c in range(CHUNKS):
             made["pre", c] = psum.tile([P, PACK, CHUNK], F32, name="pre%d" % c, tag="pre%d" % c)
             first_layer_passes(c, w2_mx, e_picked[:, span(c)], e_picked_scales[E_ROW:P, span(c)], True)
 
-        w1_src = w1_raw[:].rearrange("p j (m t) -> p m j t", t=PACK)
-        w1_halves = [sbuf([P, HIDDEN * 2], BF16, name) for name in ("w1_rounded_first", "w1_rounded")]
-        w1_dst = [half[:].rearrange("p (t m j) -> p m j t", t=2, j=PACK) for half in w1_halves]
-        nc.vector.tensor_copy(out=w1_dst[0], in_=w1_src[:, :, :, 0:2])
-        nc.vector.tensor_copy(out=w1_dst[1][:, 0:W1_ON_VECTOR], in_=w1_src[:, 0:W1_ON_VECTOR, :, 2:4])
-        nc.scalar.copy(out=w1_dst[1][:, W1_ON_VECTOR:P], in_=w1_src[:, W1_ON_VECTOR:P, :, 2:4])
-        w1_mx = sbuf([P, HIDDEN], U32, "w1_codes"), sbuf([P, HIDDEN], U8, "w1_scales")
-        for i, half in enumerate(w1_halves):
-            columns = span(i, 2 * P)
-            nc.vector.quantize_mx(out=w1_mx[0][:, columns].bitcast(FP8X4), scales=w1_mx[1][:, columns], in_=half[:])
+        w1_mx = quantise_weight(round_and_deal_weight(w1_raw, "w1", W1_ON_VECTOR), "w1")
         w3_dealt_scales = sbuf([P, HIDDEN], U8, "w3_dealt_scales", after="w1_rounded")
         deal_columns(w3_dealt_scales, w3_scale_rows)
         w3_codes = sbuf([P, HIDDEN], U32, "w3_codes")
@@ -172,16 +168,15 @@ def tile_picked_zhwy_gelu_po_kernel(
         out_rows = out_0.rearrange("(p t) c -> p t c", t=PACK)
         out_scales = sbuf([P, POSITIONS], U8, "out_scales")
 
-        out_rounded = [sbuf([P, 2 * CHUNK * PACK], BF16, "out_rounded%d" % i) for i in range(2)]
+        out_rounded = [sbuf([P, chunks * CHUNK * PACK], BF16, "out_rounded%d" % chunks) for chunks in (3, 1)]
 
         def chunk_tile(what, c, dtype):
             shape = [P, PACK, CHUNK] if dtype == F32 else [P, CHUNK * PACK]
             made[what, c] = sbuf(shape, dtype, "%s%d" % (what, c))
             return made[what, c]
 
-        def parts(c, halved=0):
-            cut = CHUNK // 2
-            return [slice(0, cut), slice(cut, CHUNK)] if c == halved else [slice(0, CHUNK)]
+        def parts(c, cut=0, count=2):
+            return [span(i, CHUNK // count) for i in range(count)] if c == cut else [slice(0, CHUNK)]
 
         def gelu(c):
             h = chunk_tile("h", c, F32)
@@ -236,24 +231,24 @@ def tile_picked_zhwy_gelu_po_kernel(
 
         def result(c):
             out = chunk_tile("out", c, F32)
-            for part in parts(c, CHUNKS - 1):
-                nc.vector.scalar_tensor_tensor(
-                    out[:, :, part], made["scaled", c, part.start][:], 0.5, skip_sb[c][:, :, part], ALU.mult, ALU.add
-                )
+            for half in parts(c, CHUNKS - 1):
+                for part in parts(c, CHUNKS - 1, LAST_PARTS):
+                    if half.start <= part.start < half.stop:
+                        scaled = made["scaled", c, half.start][:, :, part.start - half.start : part.stop - half.start]
+                        nc.vector.scalar_tensor_tensor(out[:, :, part], scaled, 0.5, skip_sb[c][:, :, part], ALU.mult, ALU.add)
             nc.sync.dma_start(out=out_rows[:, :, span(c)], in_=out[:])
 
         def round_out(c):
-            rounded, out = out_rounded[c // 2][:, span(c % 2, CHUNK * PACK)], made["out", c]
-            for part in parts(c, CHUNKS - 1):
+            rounded, out = out_rounded[c // 3][:, span(c % 3, CHUNK * PACK)], made["out", c]
+            for part in parts(c, CHUNKS - 1, LAST_PARTS):
                 round_and_interleave(False, rounded[:, part.start * PACK : part.stop * PACK], out[:, :, part])
 
         def quantise_out(first, chunks):
             columns = slice(first * CHUNK, (first + chunks) * CHUNK)
-            start = (first % 2) * CHUNK * PACK
             nc.vector.quantize_mx(
                 out=out_codes[:, columns].bitcast(FP8X4),
                 scales=out_scales[:, columns],
-                in_=out_rounded[first // 2][:, start : start + chunks * CHUNK * PACK],
+                in_=out_rounded[first // 3][:],
             )
 
         pipeline = [(step, 0) for step in (gelu, round_h, diff, gate)]
@@ -265,7 +260,7 @@ def tile_picked_zhwy_gelu_po_kernel(
         for c in range(CHUNKS):
             round_out(c)
         out_codes = sbuf([P, POSITIONS], U32, "out_codes", after="scaled%d_0" % (CHUNKS - 1))
-        for first, chunks in ((0, 2), (2, 1), (3, 1)):
+        for first, chunks in ((0, 3), (3, 1)):
             quantise_out(first, chunks)
         nc.sync.dma_start(out=words_view(out_1), in_=out_codes[:].bitcast(I32))
 

@@ -26,7 +26,6 @@ H_CHUNKS_ON_VECTOR = 2
 GATE_LAG, RESULT_LAG = 2, 3
 LAST_PARTS = 4
 X_PIECES = (1, 1, 2)
-SKIP_PIECES = (1, 1, 1, 1)
 
 
 def tile_picked_zhwy_gelu_po_kernel(
@@ -116,11 +115,14 @@ def tile_picked_zhwy_gelu_po_kernel(
         w3_words_raw = load_words(w3_words, HIDDEN, "w3_words_raw")
         skip_rows = skip.rearrange("(p t) c -> p t c", t=PACK)
         skip_sb = []
-        for chunks in SKIP_PIECES:
-            first = len(skip_sb)
-            piece = sbuf([P, PACK, chunks * CHUNK], F32, "skip%d" % first)
-            nc.sync.dma_start(out=piece[:], in_=skip_rows[:, :, first * CHUNK : (first + chunks) * CHUNK])
-            skip_sb.extend(piece[:, :, span(c)] for c in range(chunks))
+        for c in range(2):
+            piece = sbuf([P, PACK, CHUNK], F32, "skip%d" % c)
+            nc.sync.dma_start(out=piece[:], in_=skip_rows[:, :, span(c)])
+            skip_sb.append(piece[:])
+        piece = sbuf([P, PACK, 2 * CHUNK], F32, "skip2")
+        for sets in (slice(0, 2), slice(2, PACK)):
+            nc.sync.dma_start(out=piece[:, sets, :], in_=skip_rows[:, sets, 2 * CHUNK : POSITIONS])
+        skip_sb.extend(piece[:, :, span(c)] for c in range(2))
 
         unread = sbuf([P, 2], F32, "unread")
         nc.vector.memset(unread[:, 0:1], 0.0)
@@ -157,13 +159,13 @@ def tile_picked_zhwy_gelu_po_kernel(
         w3_src = w3_words_raw[:].rearrange("p (m t) -> p m t", t=PACK)
         w3_dst = w3_codes[:].rearrange("p (t m) -> p m t", t=PACK)
         nc.scalar.copy(out=w3_dst[:, :, 0:2], in_=w3_src[:, :, 0:2])
-        nc.gpsimd.tensor_copy(out=w3_dst[:, :, 2:4].rearrange("p m t -> p t m"), in_=w3_src[:, :, 2:4].rearrange("p m t -> p t m"))
         first = 0
         for chunks in X_PIECES:
             x_picked = gather(x_word_table, offs_sb, first, chunks, U32, "x_picked%d" % first)
             for c in range(chunks):
                 first_layer_passes(first + c, w1_mx, x_picked[:, span(c)], x_picked_scales[X_ROW:P, span(first + c)], False)
             first = first + chunks
+        nc.vector.tensor_copy(out=w3_dst[:, :, 2:4], in_=w3_src[:, :, 2:4])
 
         out_rows = out_0.rearrange("(p t) c -> p t c", t=PACK)
         out_scales = sbuf([P, POSITIONS], U8, "out_scales")
@@ -219,7 +221,14 @@ def tile_picked_zhwy_gelu_po_kernel(
 
         def diff(c):
             if c >= H_CHUNKS_ON_VECTOR:
-                nc.vector.tensor_tensor(chunk_tile("diff", c, F32)[:], made["h", c][:], skip_sb[c], ALU.subtract)
+                sets = slice(0, 2 if c == 2 else PACK)
+                difference = chunk_tile("diff", c, F32)
+                nc.vector.tensor_tensor(difference[:, sets, :], made["h", c][:, sets, :], skip_sb[c][:, sets, :], ALU.subtract)
+
+        def diff_rest(c):
+            if c == 2:
+                sets = slice(2, PACK)
+                nc.vector.tensor_tensor(made["diff", c][:, sets, :], made["h", c][:, sets, :], skip_sb[c][:, sets, :], ALU.subtract)
 
         def scale(c):
             for part in parts(c, CHUNKS - 1):
@@ -251,7 +260,7 @@ def tile_picked_zhwy_gelu_po_kernel(
                 in_=out_rounded[first // 3][:],
             )
 
-        pipeline = [(step, 0) for step in (gelu, round_h, diff, gate)]
+        pipeline = [(step, 0) for step in (gelu, round_h, diff, gate, diff_rest)]
         pipeline.extend([(tanh, GATE_LAG), (result, RESULT_LAG), (scale, GATE_LAG)])
         for tick in range(CHUNKS + RESULT_LAG):
             for step, lag in pipeline:

@@ -23,7 +23,7 @@ FLOPS = 3 * 2 * 512 * HIDDEN * POSITIONS
 X_ROW, E_ROW, W3_ROW = 0, 4, 8
 W1_ON_VECTOR, W2_ON_VECTOR = 32, 0
 H_CHUNKS_ON_VECTOR = 2
-GATE_LAG, RESULT_LAG = 2, 3
+ALL_SETS, FIRST_SETS, SECOND_SETS = slice(0, 4), slice(0, 2), slice(2, 4)
 LAST_PARTS = 4
 X_PIECES = (1, 1, 2)
 
@@ -180,18 +180,17 @@ def tile_picked_zhwy_gelu_po_kernel(
         def parts(c, cut=0, count=2):
             return [span(i, CHUNK // count) for i in range(count)] if c == cut else [slice(0, CHUNK)]
 
-        def gelu(c):
-            h = chunk_tile("h", c, F32)
-            for part in parts(c):
-                nc.scalar.activation(h[:, :, part], made["pre", c][:, :, part], ACT.Gelu_apprx_tanh)
+        def gelu(c, sets=ALL_SETS, part=slice(0, CHUNK)):
+            if ("h", c) not in made:
+                chunk_tile("h", c, F32)
+            nc.scalar.activation(made["h", c][:, sets, part], made["pre", c][:, sets, part], ACT.Gelu_apprx_tanh)
 
-        def round_h(c):
-            h_rounded = chunk_tile("h_rounded", c, BF16)
+        def round_h(c, part=slice(0, CHUNK)):
+            if ("h_rounded", c) not in made:
+                chunk_tile("h_rounded", c, BF16)
+            h_rounded = made["h_rounded", c]
             if c < H_CHUNKS_ON_VECTOR:
-                difference = chunk_tile("diff", c, F32)
-                for part in parts(c):
-                    round_and_interleave(True, h_rounded[:, part.start * PACK : part.stop * PACK], made["h", c][:, :, part])
-                    nc.vector.tensor_tensor(difference[:, :, part], made["h", c][:, :, part], skip_sb[c][:, :, part], ALU.subtract)
+                round_and_interleave(True, h_rounded[:, part.start * PACK : part.stop * PACK], made["h", c][:, :, part])
             else:
                 nc.scalar.activation(
                     h_rounded[:].rearrange("p (j t) -> p j t", t=PACK),
@@ -219,16 +218,12 @@ def tile_picked_zhwy_gelu_po_kernel(
         def tanh(c):
             nc.scalar.activation(chunk_tile("tanh", c, F32)[:], made["z", c][:], ACT.Tanh, scale=0.5)
 
-        def diff(c):
-            if c >= H_CHUNKS_ON_VECTOR:
-                sets = slice(0, 2 if c == 2 else PACK)
-                difference = chunk_tile("diff", c, F32)
-                nc.vector.tensor_tensor(difference[:, sets, :], made["h", c][:, sets, :], skip_sb[c][:, sets, :], ALU.subtract)
-
-        def diff_rest(c):
-            if c == 2:
-                sets = slice(2, PACK)
-                nc.vector.tensor_tensor(made["diff", c][:, sets, :], made["h", c][:, sets, :], skip_sb[c][:, sets, :], ALU.subtract)
+        def diff(c, sets=ALL_SETS, part=slice(0, CHUNK)):
+            if ("diff", c) not in made:
+                chunk_tile("diff", c, F32)
+            nc.vector.tensor_tensor(
+                made["diff", c][:, sets, part], made["h", c][:, sets, part], skip_sb[c][:, sets, part], ALU.subtract
+            )
 
         def scale(c):
             for part in parts(c, CHUNKS - 1):
@@ -260,12 +255,34 @@ def tile_picked_zhwy_gelu_po_kernel(
                 in_=out_rounded[first // 3][:],
             )
 
-        pipeline = [(step, 0) for step in (gelu, round_h, diff, gate, diff_rest)]
-        pipeline.extend([(tanh, GATE_LAG), (result, RESULT_LAG), (scale, GATE_LAG)])
-        for tick in range(CHUNKS + RESULT_LAG):
-            for step, lag in pipeline:
-                if 0 <= tick - lag < CHUNKS:
-                    step(tick - lag)
+        for half in parts(0):
+            gelu(0, part=half)
+        quarter = CHUNK // 4
+        for half, part in zip(parts(0), (slice(0, quarter), slice(quarter, 3 * quarter))):
+            round_h(0, half)
+            diff(0, part=part)
+        gate(0)
+        diff(0, part=slice(3 * quarter, CHUNK))
+        for step in (gelu, round_h, diff, gate):
+            step(1)
+        gelu(2)
+        round_h(2)
+        diff(2, FIRST_SETS)
+        gate(2)
+        diff(2, SECOND_SETS)
+        gelu(3, FIRST_SETS)
+        diff(3, FIRST_SETS)
+        tanh(0)
+        scale(0)
+        gelu(3, SECOND_SETS)
+        round_h(3)
+        diff(3, SECOND_SETS)
+        gate(3)
+        for c in range(1, CHUNKS):
+            tanh(c)
+            result(c - 1)
+            scale(c)
+        result(CHUNKS - 1)
         for c in range(CHUNKS):
             round_out(c)
         out_codes = sbuf([P, POSITIONS], U32, "out_codes", after="scaled%d_0" % (CHUNKS - 1))

@@ -21,7 +21,7 @@ FLOPS = 3 * 2 * 512 * HIDDEN * POSITIONS
 
 
 X_ROW, E_ROW, W3_ROW = 0, 4, 8
-W1_ON_VECTOR, W2_ON_VECTOR = 32, 0
+W1_ON_VECTOR, W2_ON_VECTOR = 48, 0
 H_CHUNKS_ON_VECTOR = 2
 ALL_SETS, FIRST_SETS, SECOND_SETS = slice(0, 4), slice(0, 2), slice(2, 4)
 LAST_PARTS = 4

from contextlib import ExitStack

import concourse.mybir as mybir

F32 = mybir.dt.float32
BF16 = mybir.dt.bfloat16
I32 = mybir.dt.int32
U32 = mybir.dt.uint32
U16 = mybir.dt.uint16
U8 = mybir.dt.uint8
FP8X4 = mybir.dt.float8_e4m3fn_x4
ACT = mybir.ActivationFunctionType
ALU = mybir.AluOpType

P = 128
PACK = 4
STATES, VOCAB, POSITIONS, HIDDEN = 2048, 1024, 512, 512
CHUNK = 128
CHUNKS = POSITIONS // CHUNK
FLOPS = 3 * 2 * 512 * HIDDEN * POSITIONS


X_ROW, E_ROW, W3_ROW = 0, 4, 8
W1_ON_VECTOR, W2_ON_VECTOR = 48, 0
H_CHUNKS_ON_VECTOR = 2
ALL_SETS, FIRST_SETS, SECOND_SETS = slice(0, 4), slice(0, 2), slice(2, 4)
LAST_PARTS = 4
X_PIECES = (1, 1, 2)


def tile_picked_zhwy_gelu_po_kernel(
    tc, x_words, x_scales, e_words, e_scales, w1, w2, w3_words, w3_scales, skip, offs, tok, out_0, out_1, out_2
):
    nc = tc.nc
    with ExitStack() as ctx:
        lists = ctx.enter_context(tc.tile_pool(name="lists", bufs=1))
        keep = ctx.enter_context(tc.tile_pool(name="keep", bufs=1))
        psum = ctx.enter_context(tc.psum_pool(name="psum", bufs=1))

        def sbuf(shape, dtype, name, after=None):
            return keep.tile(shape, dtype, name=name, tag=after or name, align_bytes=64)

        def span(i, width=CHUNK):
            return slice(i * width, (i + 1) * width)

        def words_view(dram):
            return dram[0].rearrange("p c r -> p (c r)").bitcast(I32)

        def load_scales(clear_on, dram, width, row, name):
            tile = sbuf([P, width], U8, name)
            clear_on.memset(tile[:].bitcast(I32), 0)
            rows = dram[0].rearrange("(q r) c -> r q c", r=4)
            for r in range(4):
                nc.sync.dma_start(out=tile[row + r : P : 32, :].bitcast(I32), in_=rows[r].bitcast(I32))
            return tile

        def load_weight(w, name):
            tile = sbuf([P, PACK, HIDDEN], F32, name)
            nc.sync.dma_start(out=tile[:], in_=w.rearrange("(p j) c -> p j c", j=PACK))
            return tile

        def load_words(dram, width, name):
            tile = sbuf([P, width], U32, name)
            nc.sync.dma_start(out=tile[:].bitcast(I32), in_=words_view(dram))
            return tile

        def round_and_deal_weight(raw, name, on_vector):
            src = raw[:].rearrange("p j (m t) -> p m j t", t=PACK)
            halves = [sbuf([P, HIDDEN * 2], BF16, name + half) for half in ("_rounded_first", "_rounded")]
            dst = [half[:].rearrange("p (t m j) -> p m j t", t=2, j=PACK) for half in halves]
            nc.vector.tensor_copy(out=dst[0], in_=src[:, :, :, 0:2])
            if on_vector:
                nc.vector.tensor_copy(out=dst[1][:, 0:on_vector], in_=src[:, 0:on_vector, :, 2:4])
            nc.scalar.copy(out=dst[1][:, on_vector:P], in_=src[:, on_vector:P, :, 2:4])
            return halves

        def quantise_weight(halves, name, after=None):
            codes = sbuf([P, HIDDEN], U32, name + "_codes")
            scales = sbuf([P, HIDDEN], U8, name + "_scales", after)
            for i, half in enumerate(halves):
                columns = span(i, 2 * P)
                nc.vector.quantize_mx(out=codes[:, columns].bitcast(FP8X4), scales=scales[:, columns], in_=half[:])
            return codes, scales

        def deal_columns(dealt, raw):
            nc.gpsimd.tensor_copy(
                out=dealt[:].rearrange("p (t m) -> p t m", t=PACK), in_=raw[:].rearrange("p (m t) -> p t m", t=PACK)
            )

        def gather(table, offsets, first_chunk, chunks, dtype, name):
            picked = sbuf([P, chunks * CHUNK], dtype, name)
            columns = slice(first_chunk * CHUNK // 16, (first_chunk + chunks) * CHUNK // 16)
            nc.vector.tensor_copy(picked[:], table[:].indirect(offsets[:, columns]))
            return picked

        def round_and_interleave(on_vector, dst, src):
            dst_view = dst.rearrange("p (c i t) -> p c t i", i=4, t=PACK)
            src_view = src.rearrange("p t (c i) -> p c t i", i=4)
            if on_vector:
                nc.vector.tensor_copy(out=dst_view, in_=src_view)
            else:
                nc.scalar.copy(out=dst_view, in_=src_view)

        offs_sb = lists.tile([P, POSITIONS // 16], U16, name="offs_sb")
        tok_sb = lists.tile([P, POSITIONS // 16], U16, name="tok_sb")
        e_word_table = load_words(e_words, VOCAB, "e_word_table")
        nc.sync.dma_start(tok_sb[:], tok)
        e_scale_table = load_scales(nc.gpsimd, e_scales, VOCAB, E_ROW, "e_scale_table")
        w2_raw = load_weight(w2, "w2_raw")
        nc.sync.dma_start(offs_sb[:], offs)
        x_scale_table = load_scales(nc.vector, x_scales, STATES, X_ROW, "x_scale_table")
        w1_raw = load_weight(w1, "w1_raw")
        w3_scale_rows = load_scales(nc.gpsimd, w3_scales, HIDDEN, W3_ROW, "w3_scale_rows")
        x_word_table = load_words(x_words, STATES, "x_word_table")
        w3_words_raw = load_words(w3_words, HIDDEN, "w3_words_raw")
        skip_rows = skip.rearrange("(p t) c -> p t c", t=PACK)
        skip_sb = []
        for c in range(2):
            piece = sbuf([P, PACK, CHUNK], F32, "skip%d" % c)
            nc.sync.dma_start(out=piece[:], in_=skip_rows[:, :, span(c)])
            skip_sb.append(piece[:])
        piece = sbuf([P, PACK, 2 * CHUNK], F32, "skip2")
        for sets in (slice(0, 2), slice(2, PACK)):
            nc.sync.dma_start(out=piece[:, sets, :], in_=skip_rows[:, sets, 2 * CHUNK : POSITIONS])
        skip_sb.extend(piece[:, :, span(c)] for c in range(2))

        unread = sbuf([P, 2], F32, "unread")
        nc.vector.memset(unread[:, 0:1], 0.0)
        nc.scalar.activation(unread[:, 1:2], unread[:, 0:1], ACT.Gelu_apprx_tanh)

        made = {}

        def first_layer_passes(c, weight, codes, scales, opens):
            w_codes, w_scales = weight
            for t in range(PACK):
                nc.tensor.matmul_mx(
                    out=made["pre", c][:, t, :],
                    lhsT=w_codes[:, span(t, P)].bitcast(FP8X4),
                    lhsT_scale=w_scales[:, span(t, P)],
                    rhs=codes.bitcast(FP8X4),
                    rhs_scale=scales,
                    start=(opens and t == 0),
                    stop=(not opens and t == PACK - 1),
                )

        e_picked = gather(e_word_table, tok_sb, 0, CHUNKS, U32, "e_picked")
        e_picked_scales = gather(e_scale_table, tok_sb, 0, CHUNKS, U8, "e_picked_scales")
        w2_rounded = round_and_deal_weight(w2_raw, "w2", W2_ON_VECTOR)
        x_picked_scales = gather(x_scale_table, offs_sb, 0, CHUNKS, U8, "x_picked_scales")
        w2_mx = quantise_weight(w2_rounded, "w2", after="x_scale_table")
        for c in range(CHUNKS):
            made["pre", c] = psum.tile([P, PACK, CHUNK], F32, name="pre%d" % c, tag="pre%d" % c)
            first_layer_passes(c, w2_mx, e_picked[:, span(c)], e_picked_scales[E_ROW:P, span(c)], True)

        w1_mx = quantise_weight(round_and_deal_weight(w1_raw, "w1", W1_ON_VECTOR), "w1")
        w3_dealt_scales = sbuf([P, HIDDEN], U8, "w3_dealt_scales", after="w1_rounded")
        deal_columns(w3_dealt_scales, w3_scale_rows)
        w3_codes = sbuf([P, HIDDEN], U32, "w3_codes")
        w3_src = w3_words_raw[:].rearrange("p (m t) -> p m t", t=PACK)
        w3_dst = w3_codes[:].rearrange("p (t m) -> p m t", t=PACK)
        nc.scalar.copy(out=w3_dst[:, :, 0:2], in_=w3_src[:, :, 0:2])
        first = 0
        for chunks in X_PIECES:
            x_picked = gather(x_word_table, offs_sb, first, chunks, U32, "x_picked%d" % first)
            for c in range(chunks):
                first_layer_passes(first + c, w1_mx, x_picked[:, span(c)], x_picked_scales[X_ROW:P, span(first + c)], False)
            first = first + chunks
        nc.vector.tensor_copy(out=w3_dst[:, :, 2:4], in_=w3_src[:, :, 2:4])

        out_rows = out_0.rearrange("(p t) c -> p t c", t=PACK)
        out_scales = sbuf([P, POSITIONS], U8, "out_scales")

        out_rounded = [sbuf([P, chunks * CHUNK * PACK], BF16, "out_rounded%d" % chunks) for chunks in (3, 1)]

        def chunk_tile(what, c, dtype):
            shape = [P, PACK, CHUNK] if dtype == F32 else [P, CHUNK * PACK]
            made[what, c] = sbuf(shape, dtype, "%s%d" % (what, c))
            return made[what, c]

        def parts(c, cut=0, count=2):
            return [span(i, CHUNK // count) for i in range(count)] if c == cut else [slice(0, CHUNK)]

        def gelu(c, sets=ALL_SETS, part=slice(0, CHUNK)):
            if ("h", c) not in made:
                chunk_tile("h", c, F32)
            nc.scalar.activation(made["h", c][:, sets, part], made["pre", c][:, sets, part], ACT.Gelu_apprx_tanh)

        def round_h(c, part=slice(0, CHUNK)):
            if ("h_rounded", c) not in made:
                chunk_tile("h_rounded", c, BF16)
            h_rounded = made["h_rounded", c]
            if c < H_CHUNKS_ON_VECTOR:
                round_and_interleave(True, h_rounded[:, part.start * PACK : part.stop * PACK], made["h", c][:, :, part])
            else:
                nc.scalar.activation(
                    h_rounded[:].rearrange("p (j t) -> p j t", t=PACK),
                    made["pre", c][:].rearrange("p t j -> p j t"),
                    ACT.Gelu_apprx_tanh,
                )

        def gate(c):
            h_codes = sbuf([P, CHUNK], U32, "h_codes%d" % c)
            h_scales = sbuf([P, CHUNK], U8, "h_scales%d" % c)
            nc.vector.quantize_mx(out=h_codes[:].bitcast(FP8X4), scales=h_scales[:], in_=made["h_rounded", c][:])
            z = psum.tile([P, PACK, CHUNK], F32, name="z%d" % c, tag="z%d" % c)
            for t in range(PACK):
                nc.tensor.matmul_mx(
                    out=z[:, t, :],
                    lhsT=w3_codes[:, span(t, P)].bitcast(FP8X4),
                    lhsT_scale=w3_dealt_scales[W3_ROW:P, span(t, P)],
                    rhs=h_codes[:].bitcast(FP8X4),
                    rhs_scale=h_scales[:],
                    start=True,
                    stop=True,
                )
            made["z", c] = z

        def tanh(c):
            nc.scalar.activation(chunk_tile("tanh", c, F32)[:], made["z", c][:], ACT.Tanh, scale=0.5)

        def diff(c, sets=ALL_SETS, part=slice(0, CHUNK)):
            if ("diff", c) not in made:
                chunk_tile("diff", c, F32)
            nc.vector.tensor_tensor(
                made["diff", c][:, sets, part], made["h", c][:, sets, part], skip_sb[c][:, sets, part], ALU.subtract
            )

        def scale(c):
            for part in parts(c, CHUNKS - 1):
                scaled = sbuf([P, PACK, part.stop - part.start], F32, "scaled%d_%d" % (c, part.start))
                made["scaled", c, part.start] = scaled
                nc.vector.scalar_tensor_tensor(
                    scaled[:], made["tanh", c][:, :, part], 1.0, made["diff", c][:, :, part], ALU.add, ALU.mult
                )

        def result(c):
            out = chunk_tile("out", c, F32)
            for half in parts(c, CHUNKS - 1):
                for part in parts(c, CHUNKS - 1, LAST_PARTS):
                    if half.start <= part.start < half.stop:
                        scaled = made["scaled", c, half.start][:, :, part.start - half.start : part.stop - half.start]
                        nc.vector.scalar_tensor_tensor(out[:, :, part], scaled, 0.5, skip_sb[c][:, :, part], ALU.mult, ALU.add)
            nc.sync.dma_start(out=out_rows[:, :, span(c)], in_=out[:])

        def round_out(c):
            rounded, out = out_rounded[c // 3][:, span(c % 3, CHUNK * PACK)], made["out", c]
            for part in parts(c, CHUNKS - 1, LAST_PARTS):
                round_and_interleave(False, rounded[:, part.start * PACK : part.stop * PACK], out[:, :, part])

        def quantise_out(first, chunks):
            columns = slice(first * CHUNK, (first + chunks) * CHUNK)
            nc.vector.quantize_mx(
                out=out_codes[:, columns].bitcast(FP8X4),
                scales=out_scales[:, columns],
                in_=out_rounded[first // 3][:],
            )

        for half in parts(0):
            gelu(0, part=half)
        quarter = CHUNK // 4
        for half, part in zip(parts(0), (slice(0, quarter), slice(quarter, 3 * quarter))):
            round_h(0, half)
            diff(0, part=part)
        gate(0)
        diff(0, part=slice(3 * quarter, CHUNK))
        for step in (gelu, round_h, diff, gate):
            step(1)
        gelu(2)
        round_h(2)
        diff(2, FIRST_SETS)
        gate(2)
        diff(2, SECOND_SETS)
        gelu(3, FIRST_SETS)
        diff(3, FIRST_SETS)
        tanh(0)
        scale(0)
        gelu(3, SECOND_SETS)
        round_h(3)
        diff(3, SECOND_SETS)
        gate(3)
        for c in range(1, CHUNKS):
            tanh(c)
            result(c - 1)
            scale(c)
        result(CHUNKS - 1)
        for c in range(CHUNKS):
            round_out(c)
        out_codes = sbuf([P, POSITIONS], U32, "out_codes", after="scaled%d_0" % (CHUNKS - 1))
        for first, chunks in ((0, 3), (3, 1)):
            quantise_out(first, chunks)
        nc.sync.dma_start(out=words_view(out_1), in_=out_codes[:].bitcast(I32))

        for q in range(4):
            queue = nc.scalar if q < 2 else nc.sync
            queue.dma_start(
                out=out_2[0, 4 * q : 4 * q + 4, :].bitcast(I32), in_=out_scales[32 * q : 32 * q + 4, :].bitcast(I32)
            )
